import numpy as np
import ml_dtypes


def mxq(x, axis, fmt="e4m3"):
    dtype, down = {"e4m3": (ml_dtypes.float8_e4m3fn, 7), "e5m2": (ml_dtypes.float8_e5m2, 14)}[fmt]
    v = np.moveaxis(np.asarray(x, np.float32).astype(ml_dtypes.bfloat16).astype(np.float64), axis, -1)
    blocks = v.reshape(v.shape[:-1] + (-1, 32))
    amax = np.abs(blocks).max(-1, keepdims=True)
    byte = np.maximum(np.where(amax > 0, np.frexp(amax)[1] - 1 + 127, 0) - down, 1)
    scale = np.exp2(byte - 127.0)
    codes = (blocks / scale).astype(np.float32).astype(dtype).astype(np.float64)
    return np.moveaxis((codes * scale).reshape(v.shape), -1, axis)


WIDE = False


def mx_kscale(k):
    if not WIDE:
        return np.ones(k)
    levels = np.array([10, -10, 5, -5, 0])
    if k % 512:
        return np.exp2(np.random.permutation(np.resize(levels, k // 32))).repeat(32)
    a = np.empty((k // 512, 16))
    for p in range(k // 512):
        a[p, :8] = np.random.permutation(np.resize(levels, 8))
        for g in range(8):
            far = levels[np.abs(levels - a[p, g]) >= 10]
            a[p, g + 8] = far[np.random.randint(len(far))]
    return np.exp2(a.ravel()).repeat(32)


def f64(x):
    return np.asarray(x).astype(np.float64)


def striped(idx):
    return np.tile(idx.reshape(-1, 16).T, (8, 1)).astype(np.uint16)


def unstriped(offs):
    return offs[:16].T.reshape(-1).astype(np.int64)


def striped8(idx):
    return np.concatenate([x.reshape(-1, 16).T for x in idx]).astype(np.uint16)


def runs(offs, k):
    lists = np.stack([offs[16 * r : 16 * r + 16].T.reshape(-1) for r in range(8)]).astype(np.int64)
    return lists[np.arange(k) % 512 // 64]


def pack_weight(w):
    k, n = w.shape
    w = f64(np.asarray(w, np.float32).astype(ml_dtypes.bfloat16)).reshape(k // 32, 32, n)
    amax = np.abs(w).max(1)
    byte = np.clip(np.where(amax > 0, np.frexp(amax)[1] - 1 + 127 - 7, 1), 1, 254)
    scaled = (w * np.exp2(127.0 - byte)[:, None, :]).reshape(k, n).astype(np.float32)
    words = np.ascontiguousarray(scaled.reshape(k // 512, 128, 4, n).transpose(0, 1, 3, 2)).astype(ml_dtypes.float8_e4m3fn).view(np.uint8)
    return words, np.ascontiguousarray(byte.astype(np.uint8).reshape(k // 512, 16, n))


def unpack_weight(words, scales):
    g, p, n, _ = words.shape
    vals = np.ascontiguousarray(words).view(ml_dtypes.float8_e4m3fn).astype(np.float64) * np.repeat(np.exp2(scales.astype(np.float64) - 127.0), 8, axis=1)[..., None]
    return vals.transpose(0, 1, 3, 2).reshape(g * 512, n)


K, T, S, N, H = 512, 2048, 512, 512, 512
P = 2 ** 7


def setup_inputs():
    n = np.random.standard_normal
    s = mx_kscale(K)[:, None]
    u = mx_kscale(H)
    packed_xT = pack_weight(n((K, T)) * s)
    return {
        "x_words": packed_xT[0],
        "x_scales": packed_xT[1],
        "w1": (n((K, H)) / np.sqrt(K) / s).astype(np.float32),
        "g1": np.tile(np.random.uniform(0.1, 0.8, S), (P, 1)).astype(np.float32),
        "g2": np.tile(np.random.uniform(0.1, 0.8, S), (P, 1)).astype(np.float32),
        "g3": np.tile(np.random.uniform(0.1, 0.8, S), (P, 1)).astype(np.float32),
        "c2": (np.random.uniform(0.5, 1.5, (H, 1)) * u[:, None]).astype(np.float32),
        "c1": (np.random.uniform(0.5, 1.5, (H, 1)) * u[:, None]).astype(np.float32),
        "w2": (n((H, N)) / np.sqrt(2 * H) / u[:, None]).astype(np.float32),
        "w3": (n((H, N)) / np.sqrt(2 * H) / u[:, None]).astype(np.float32),
        "offs": striped(np.random.permutation(T)[:S]),
        "p1": striped8(np.stack([np.random.permutation(S) for _ in range(8)])),
        "p2": striped8(np.stack([np.random.permutation(S) for _ in range(8)])),
        "p3": striped8(np.stack([np.random.permutation(S) for _ in range(8)])),
    }


def reference(x_words, x_scales, w1, g1, g2, g3, c2, c1, w2, w3, offs, p1, p2, p3):
    xq = unpack_weight(x_words, x_scales)[:, unstriped(offs)]
    y = mxq(f64(w1), 0, "e4m3").T @ xq
    a = f64(g1)[:1] * (y[np.arange(H)[:, None], runs(p1, H)]) + f64(g2)[:1] * (y[np.arange(H)[:, None], runs(p2, H)]) + f64(g3)[:1] * (y[np.arange(H)[:, None], runs(p3, H)])
    z2 = f64(c1) * a
    z = f64(c2) * ((a) ** 2)
    return mxq(f64(w2), 0, "e4m3").T @ mxq(z2, 0, "e4m3") + mxq(f64(w3), 0, "e4m3").T @ mxq(z, 0, "e4m3")

@@ -1,0 +1,236 @@
+from contextlib import ExitStack
+
+import concourse.mybir as mybir
+from concourse.masks import make_identity
+
+K, T, S, N, H = 512, 2048, 512, 512, 512
+FLOPS = 2 * K * H * S + 2 * 2 * H * N * S
+
+F32 = mybir.dt.float32
+BF16 = mybir.dt.bfloat16
+I32 = mybir.dt.int32
+U32 = mybir.dt.uint32
+U16 = mybir.dt.uint16
+U8 = mybir.dt.uint8
+FP8X4 = mybir.dt.float8_e4m3fn_x4
+MULT = mybir.AluOpType.mult
+ADD = mybir.AluOpType.add
+COPY = mybir.ActivationFunctionType.Copy
+SQUARE = mybir.ActivationFunctionType.Square
+
+P = 128
+PACK = 4
+CH = 128
+CHUNKS = S // CH
+HALF = S // 2
+
+
+def tile_picked_ace8_none_p_kernel(
+    tc, x_words, x_scales, w1, g1, g2, g3, c2, c1, w2, w3, offs, p1, p2, p3, out
+):
+    nc = tc.nc
+    with ExitStack() as ctx:
+        keep = ctx.enter_context(tc.tile_pool(name="keep", bufs=1))
+        ring = ctx.enter_context(tc.tile_pool(name="ring", bufs=2))
+        terms_pool = ctx.enter_context(tc.tile_pool(name="terms", bufs=6))
+        psum = ctx.enter_context(tc.psum_pool(name="psum", bufs=1))
+
+        def bank(b, shape):
+            return psum.tile(shape, F32, name=f"bank{b}", tag=f"bank{b}")
+
+        xs = keep.tile([P, T], U8, name="xs", align_bytes=64)
+        nc.gpsimd.memset(xs[:].bitcast(I32), 0)
+        w1_raw = keep.tile([P, PACK, H], F32, name="w1_raw")
+        nc.sync.dma_start(w1_raw[:], w1.rearrange("(p j) c -> p j c", j=PACK))
+        offs_t = keep.tile([P, S // 16], U16, name="offs_t")
+        nc.sync.dma_start(offs_t[:], offs)
+        for q in range(4):
+            nc.sync.dma_start(
+                xs[32 * q : 32 * q + 4, :].bitcast(I32), x_scales[0, 4 * q : 4 * q + 4, :].bitcast(I32)
+            )
+        xw = keep.tile([P, T], I32, name="xw", align_bytes=64)
+        nc.sync.dma_start(xw[:], x_words[0].rearrange("p n t -> p (n t)").bitcast(I32))
+
+        lists, gains = [], []
+        for k, (pk, gk) in enumerate(((p1, g1), (p2, g2), (p3, g3))):
+            lt = keep.tile([P, S // 16], U16, name=f"list{k}")
+            nc.sync.dma_start(lt[:], pk)
+            gt = keep.tile([P, S], F32, name=f"gain{k}")
+            nc.sync.dma_start(gt[:], gk)
+            lists.append(lt)
+            gains.append(gt)
+        c1_t = keep.tile([P, PACK], F32, name="c1_t")
+        nc.sync.dma_start(c1_t[:], c1.rearrange("(p t) o -> p (t o)", t=PACK))
+        c2_t = keep.tile([P, PACK], F32, name="c2_t")
+        nc.sync.dma_start(c2_t[:], c2.rearrange("(p t) o -> p (t o)", t=PACK))
+        w_raw = []
+        for i, w in enumerate((w2, w3)):
+            wr = keep.tile([P, PACK, N], F32, name=f"w_raw{i}", tag=f"w_raw{i}")
+            nc.sync.dma_start(wr[:], w.rearrange("(p j) c -> p j c", j=PACK))
+            w_raw.append(wr)
+
+        ident = keep.tile([P, P], F32, name="ident")
+        make_identity(nc, ident[:])
+
+        w1_b = keep.tile([P, PACK, P, PACK], BF16, name="w1_b", align_bytes=64)
+        src = w1_raw[:].rearrange("p j (m t) -> p m t j", t=PACK)
+        dst = w1_b[:].rearrange("p t m j -> p m t j")
+        nc.vector.tensor_copy(dst[:, :, 0:2, :], src[:, :, 0:2, :])
+        nc.scalar.copy(dst[:, :, 2:4, :], src[:, :, 2:4, :])
+        xs_g = keep.tile([P, S], U8, name="xs_g", align_bytes=64)
+        nc.vector.tensor_copy(xs_g[:], xs[:].indirect(offs_t[:]))
+        w1_q = keep.tile([P, H], U32, name="w1_q", align_bytes=64)
+        w1_s = keep.tile([P, H], U8, name="w1_s", align_bytes=64)
+        nc.vector.quantize_mx(
+            out=w1_q[:].bitcast(FP8X4), scales=w1_s[:], in_=w1_b[:].rearrange("p t m j -> p (t m j)")
+        )
+
+        xw_g = keep.tile([P, S], U32, name="xw_g", align_bytes=64)
+        for h in range(2):
+            nc.vector.tensor_copy(
+                xw_g[:, h * HALF : (h + 1) * HALF],
+                xw[:].bitcast(U32).indirect(offs_t[:, h * 16 : (h + 1) * 16]),
+            )
+
+        def first_product(ps, t, cols):
+            nc.tensor.matmul_mx(
+                out=ps,
+                lhsT=w1_q[:, t * P : (t + 1) * P].bitcast(FP8X4),
+                lhsT_scale=w1_s[:, t * P : (t + 1) * P],
+                rhs=xw_g[:, cols].bitcast(FP8X4),
+                rhs_scale=xs_g[:, cols],
+                start=True,
+                stop=True,
+            )
+
+        y = [keep.tile([P, S], F32, name=f"y{t}") for t in range(PACK)]
+        for h in range(2):
+            cols = slice(h * HALF, (h + 1) * HALF)
+            ps = bank(4 * h, [P, HALF])
+            first_product(ps[:], 0, cols)
+            if h == 0:
+                nc.scalar.copy(y[0][:, cols], ps[:])
+            else:
+                nc.vector.tensor_copy(y[0][:, cols], ps[:])
+        for t in range(1, PACK):
+            ps = bank(t, [P, S])
+            first_product(ps[:], t, slice(0, S))
+            nc.scalar.copy(y[t][:], ps[:])
+
+        w_q, w_s = [], []
+        for i in range(2):
+            wb = keep.tile([P, N, PACK], BF16, name=f"w_b{i}", align_bytes=64)
+            for h in range(4):
+                cols = slice(h * P, (h + 1) * P)
+                nc.scalar.copy(
+                    wb[:, cols, :].rearrange("p (c i) t -> p c t i", i=4),
+                    w_raw[i][:, :, cols].rearrange("p t (c i) -> p c t i", i=4),
+                )
+            wq = keep.tile([P, N], U32, name=f"w_q{i}", align_bytes=64)
+            ws = keep.tile([P, N], U8, name=f"w_s{i}", align_bytes=64)
+            nc.vector.quantize_mx(
+                out=wq[:].bitcast(FP8X4), scales=ws[:], in_=wb[:].rearrange("p m t -> p (m t)")
+            )
+            w_q.append(wq)
+            w_s.append(ws)
+
+        out_v = out.rearrange("(a p) j -> p a j", p=P)
+
+        def gather(c, t, k):
+            term = terms_pool.tile([P, CH], F32, name="term")
+            nc.vector.tensor_tensor(
+                term[:],
+                y[t][:].indirect(lists[k][:, c * (CH // 16) : (c + 1) * (CH // 16)]),
+                gains[k][:, c * CH : (c + 1) * CH],
+                MULT,
+            )
+            return term
+
+        def front_pe(c, zz, planes):
+            at_ps = bank(4 + c % 2, [P, planes, P])
+            for t in range(planes):
+                for k in range(3):
+                    term = gather(c, t, k)
+                    nc.tensor.matmul(
+                        at_ps[:, t, :], term[:], ident[:], start=(k == 0), stop=(k == 2), is_transpose=True
+                    )
+            at_sb = ring.tile([P, planes, P], F32, name="at_sb")
+            nc.scalar.copy(at_sb[:], at_ps[:])
+            a_ps = bank(6 + c % 2, [P, planes, CH])
+            for t in range(planes):
+                nc.tensor.transpose(a_ps[:, t, :], at_sb[:, t, :], ident[:])
+            sq = ring.tile([P, planes, CH], F32, name="sq")
+            nc.scalar.activation(sq[:], a_ps[:], SQUARE)
+            for t in range(planes):
+                nc.scalar.activation(zz[:, t, 0:CH], a_ps[:, t, :], COPY, scale=c1_t[:, t : t + 1])
+            for t in range(planes):
+                nc.scalar.activation(zz[:, t, CH : 2 * CH], sq[:, t, :], COPY, scale=c2_t[:, t : t + 1])
+
+        def front_direct(c, zz, first):
+            part = ring.tile([P, PACK, CH], F32, name="part")
+            a_sb = ring.tile([P, PACK, CH], F32, name="a_sb")
+
+            def finish(t, term):
+                nc.vector.tensor_tensor(a_sb[:, t, :], part[:, t, :], term[:], ADD)
+                nc.scalar.activation(zz[:, t, 0:CH], a_sb[:, t, :], COPY, scale=c1_t[:, t : t + 1])
+
+            def second(t):
+                nc.vector.scalar_tensor_tensor(
+                    zz[:, t, CH : 2 * CH], a_sb[:, t, :], c2_t[:, t : t + 1], a_sb[:, t, :], MULT, MULT
+                )
+
+            last = None
+            for t in range(first, PACK):
+                term0 = gather(c, t, 0)
+                if last is not None:
+                    finish(t - 1, last)
+                term1 = gather(c, t, 1)
+                if last is not None:
+                    second(t - 1)
+                last = gather(c, t, 2)
+                nc.vector.tensor_tensor(part[:, t, :], term0[:], term1[:], ADD)
+            finish(PACK - 1, last)
+            second(PACK - 1)
+
+        def back(c, zz):
+            zi = ring.tile([P, 2 * CH, PACK], BF16, name="zi", align_bytes=64)
+            dst = zi[:].rearrange("p (c i) t -> p c t i", i=4)
+            src = zz[:].rearrange("p t (c i) -> p c t i", i=4)
+            if c < 2:
+                nc.scalar.copy(dst, src)
+            else:
+                nc.vector.tensor_copy(dst, src)
+            zq = ring.tile([P, 2 * CH], U32, name="zq", align_bytes=64)
+            zs = ring.tile([P, 2 * CH], U8, name="zs", align_bytes=64)
+            nc.vector.quantize_mx(out=zq[:].bitcast(FP8X4), scales=zs[:], in_=zi[:].rearrange("p j t -> p (j t)"))
+            for half in range(2):
+                o_ps = bank(2 * (c % 2) + half, [P, 2, CH])
+                for a in range(2):
+                    rows = slice((2 * half + a) * P, (2 * half + a + 1) * P)
+                    for i in range(2):
+                        nc.tensor.matmul_mx(
+                            out=o_ps[:, a, :],
+                            lhsT=w_q[i][:, rows].bitcast(FP8X4),
+                            lhsT_scale=w_s[i][:, rows],
+                            rhs=zq[:, i * CH : (i + 1) * CH].bitcast(FP8X4),
+                            rhs_scale=zs[:, i * CH : (i + 1) * CH],
+                            start=(i == 0),
+                            stop=(i == 1),
+                        )
+                o_sb = ring.tile([P, 2, CH], F32, name="o_sb", tag=f"o_sb{half}")
+                if c == CHUNKS - 1 and half == 1:
+                    nc.vector.tensor_copy(o_sb[:], o_ps[:])
+                else:
+                    nc.scalar.copy(o_sb[:], o_ps[:])
+                nc.sync.dma_start(out_v[:, 2 * half : 2 * half + 2, c * CH : (c + 1) * CH], o_sb[:])
+
+        zz = [keep.tile([P, PACK, 2 * CH], BF16, name=f"zz{c}") for c in range(CHUNKS)]
+        front_pe(0, zz[0], PACK)
+        front_pe(1, zz[1], PACK)
+        back(0, zz[0])
+        front_pe(2, zz[2], PACK)
+        back(1, zz[1])
+        front_pe(3, zz[3], 2)
+        back(2, zz[2])
+        front_direct(3, zz[3], 2)
+        back(3, zz[3])

@@ -20,9 +20,9 @@ SQUARE = mybir.ActivationFunctionType.Square
 
 P = 128
 PACK = 4
-CH = 128
-CHUNKS = S // CH
 HALF = S // 2
+TERM_SLOTS = 4
+BLOCKS = ((0, 128), (128, 256), (384, 128))
 
 
 def tile_picked_ace8_none_p_kernel(
@@ -32,65 +32,77 @@ def tile_picked_ace8_none_p_kernel(
     with ExitStack() as ctx:
         keep = ctx.enter_context(tc.tile_pool(name="keep", bufs=1))
         ring = ctx.enter_context(tc.tile_pool(name="ring", bufs=2))
-        terms_pool = ctx.enter_context(tc.tile_pool(name="terms", bufs=6))
         psum = ctx.enter_context(tc.psum_pool(name="psum", bufs=1))
 
         def bank(b, shape):
             return psum.tile(shape, F32, name=f"bank{b}", tag=f"bank{b}")
 
+        def load_list(name, src):
+            lt = keep.tile([P, S // 16], U16, name=name)
+            nc.sync.dma_start(lt[:], src)
+            return lt
+
+        def load_gain(name, src):
+            gt = keep.tile([P, S], F32, name=name)
+            nc.sync.dma_start(gt[:], src)
+            return gt
+
+        def load_rows(name, src):
+            wr = keep.tile([P, PACK, src.shape[1]], F32, name=name, tag=name)
+            nc.sync.dma_start(wr[:], src.rearrange("(p j) c -> p j c", j=PACK))
+            return wr
+
         xs = keep.tile([P, T], U8, name="xs", align_bytes=64)
         nc.gpsimd.memset(xs[:].bitcast(I32), 0)
-        w1_raw = keep.tile([P, PACK, H], F32, name="w1_raw")
-        nc.sync.dma_start(w1_raw[:], w1.rearrange("(p j) c -> p j c", j=PACK))
-        offs_t = keep.tile([P, S // 16], U16, name="offs_t")
-        nc.sync.dma_start(offs_t[:], offs)
+        offs_t = load_list("offs_t", offs)
+        lists = [load_list("list0", p1), load_list("list1", p2)]
+        xw = keep.tile([P, T], I32, name="xw", align_bytes=64)
+        nc.sync.dma_start(xw[:], x_words[0].rearrange("p n t -> p (n t)").bitcast(I32))
+        lists.append(load_list("list2", p3))
+        c1_t = keep.tile([P, PACK], F32, name="c1_t")
+        nc.sync.dma_start(c1_t[:], c1.rearrange("(p t) o -> p (t o)", t=PACK))
         for q in range(4):
             nc.sync.dma_start(
                 xs[32 * q : 32 * q + 4, :].bitcast(I32), x_scales[0, 4 * q : 4 * q + 4, :].bitcast(I32)
             )
-        xw = keep.tile([P, T], I32, name="xw", align_bytes=64)
-        nc.sync.dma_start(xw[:], x_words[0].rearrange("p n t -> p (n t)").bitcast(I32))
-
-        lists, gains = [], []
-        for k, (pk, gk) in enumerate(((p1, g1), (p2, g2), (p3, g3))):
-            lt = keep.tile([P, S // 16], U16, name=f"list{k}")
-            nc.sync.dma_start(lt[:], pk)
-            gt = keep.tile([P, S], F32, name=f"gain{k}")
-            nc.sync.dma_start(gt[:], gk)
-            lists.append(lt)
-            gains.append(gt)
-        c1_t = keep.tile([P, PACK], F32, name="c1_t")
-        nc.sync.dma_start(c1_t[:], c1.rearrange("(p t) o -> p (t o)", t=PACK))
+        w1_raw = load_rows("w1_raw", w1)
+        gains = [load_gain("gain0", g1), load_gain("gain1", g2), load_gain("gain2", g3)]
         c2_t = keep.tile([P, PACK], F32, name="c2_t")
         nc.sync.dma_start(c2_t[:], c2.rearrange("(p t) o -> p (t o)", t=PACK))
-        w_raw = []
-        for i, w in enumerate((w2, w3)):
-            wr = keep.tile([P, PACK, N], F32, name=f"w_raw{i}", tag=f"w_raw{i}")
-            nc.sync.dma_start(wr[:], w.rearrange("(p j) c -> p j c", j=PACK))
-            w_raw.append(wr)
+        w_raw = [load_rows("w2_raw", w2), load_rows("w3_raw", w3)]
 
         ident = keep.tile([P, P], F32, name="ident")
         make_identity(nc, ident[:])
 
-        w1_b = keep.tile([P, PACK, P, PACK], BF16, name="w1_b", align_bytes=64)
-        src = w1_raw[:].rearrange("p j (m t) -> p m t j", t=PACK)
-        dst = w1_b[:].rearrange("p t m j -> p m t j")
-        nc.vector.tensor_copy(dst[:, :, 0:2, :], src[:, :, 0:2, :])
-        nc.scalar.copy(dst[:, :, 2:4, :], src[:, :, 2:4, :])
-        xs_g = keep.tile([P, S], U8, name="xs_g", align_bytes=64)
-        nc.vector.tensor_copy(xs_g[:], xs[:].indirect(offs_t[:]))
-        w1_q = keep.tile([P, H], U32, name="w1_q", align_bytes=64)
-        w1_s = keep.tile([P, H], U8, name="w1_s", align_bytes=64)
-        nc.vector.quantize_mx(
-            out=w1_q[:].bitcast(FP8X4), scales=w1_s[:], in_=w1_b[:].rearrange("p t m j -> p (t m j)")
-        )
+        y = [keep.tile([P, 2 * S if t < PACK - 1 else S], F32, name=f"y{t}") for t in range(PACK)]
+        for t in range(PACK - 1):
+            nc.gpsimd.memset(y[t][:, S : 2 * S], 0.0)
 
         xw_g = keep.tile([P, S], U32, name="xw_g", align_bytes=64)
-        for h in range(2):
-            nc.vector.tensor_copy(
-                xw_g[:, h * HALF : (h + 1) * HALF],
-                xw[:].bitcast(U32).indirect(offs_t[:, h * 16 : (h + 1) * 16]),
+        nc.vector.tensor_copy(xw_g[:], xw[:].bitcast(U32).indirect(offs_t[:]))
+        xs_g = keep.tile([P, S], U8, name="xs_g", align_bytes=64)
+        nc.vector.tensor_copy(xs_g[:], xs[:].indirect(offs_t[:]))
+
+        w1_b = keep.tile([P, PACK, P, PACK], BF16, name="w1_b", align_bytes=64)
+        w1_q = keep.tile([P, H], U32, name="w1_q", align_bytes=64)
+        w1_s = keep.tile([P, H], U8, name="w1_s", align_bytes=64)
+        src = w1_raw[:].rearrange("p j (m t) -> p m t j", t=PACK)
+        dst = w1_b[:].rearrange("p t m j -> p m t j")
+
+        def quantize_w1(first, count):
+            cols = slice(first * P, (first + count) * P)
+            nc.vector.quantize_mx(
+                out=w1_q[:, cols].bitcast(FP8X4),
+                scales=w1_s[:, cols],
+                in_=w1_b[:, first : first + count].rearrange("p t m j -> p (t m j)"),
             )
+
+        nc.vector.tensor_copy(dst[:, :, 0, :], src[:, :, 0, :])
+        nc.scalar.copy(dst[:, :, 1, :], src[:, :, 1, :])
+        quantize_w1(0, 1)
+        nc.vector.tensor_copy(dst[:, :, 2:4, :], src[:, :, 2:4, :])
+        quantize_w1(1, 1)
+        quantize_w1(2, 2)
 
         def first_product(ps, t, cols):
             nc.tensor.matmul_mx(
@@ -103,22 +115,19 @@ def tile_picked_ace8_none_p_kernel(
                 stop=True,
             )
 
-        y = [keep.tile([P, S], F32, name=f"y{t}") for t in range(PACK)]
-        for h in range(2):
+        for h, copy in enumerate((nc.scalar.copy, nc.vector.tensor_copy)):
             cols = slice(h * HALF, (h + 1) * HALF)
-            ps = bank(4 * h, [P, HALF])
+            ps = bank(h, [P, HALF])
             first_product(ps[:], 0, cols)
-            if h == 0:
-                nc.scalar.copy(y[0][:, cols], ps[:])
-            else:
-                nc.vector.tensor_copy(y[0][:, cols], ps[:])
+            copy(y[0][:, cols], ps[:])
         for t in range(1, PACK):
-            ps = bank(t, [P, S])
+            ps = bank((6, 7, 0)[t - 1], [P, S])
             first_product(ps[:], t, slice(0, S))
-            nc.scalar.copy(y[t][:], ps[:])
+            nc.scalar.copy(y[t][:, 0:S], ps[:])
 
         w_q, w_s = [], []
-        for i in range(2):
+
+        def last_weights(i):
             wb = keep.tile([P, N, PACK], BF16, name=f"w_b{i}", align_bytes=64)
             for h in range(4):
                 cols = slice(h * P, (h + 1) * P)
@@ -135,76 +144,68 @@ def tile_picked_ace8_none_p_kernel(
             w_s.append(ws)
 
         out_v = out.rearrange("(a p) j -> p a j", p=P)
+        zz = keep.tile([P, PACK, 2, S], BF16, name="zz")
 
-        def gather(c, t, k):
-            term = terms_pool.tile([P, CH], F32, name="term")
+        def gather(t, k, first, width, tag):
+            term = keep.tile([P, width], F32, name="term", tag=tag, align_bytes=64)
             nc.vector.tensor_tensor(
                 term[:],
-                y[t][:].indirect(lists[k][:, c * (CH // 16) : (c + 1) * (CH // 16)]),
-                gains[k][:, c * CH : (c + 1) * CH],
+                y[t][:].indirect(lists[k][:, first // 16 : (first + width) // 16]),
+                gains[k][:, first : first + width],
                 MULT,
             )
             return term
 
-        def front_pe(c, zz, planes):
-            at_ps = bank(4 + c % 2, [P, planes, P])
-            for t in range(planes):
-                for k in range(3):
-                    term = gather(c, t, k)
+        def plane_by_transposes(t):
+            at_ps = [bank(2 + b, [P, P]) for b in range(4)]
+            for k in range(3):
+                term = gather(t, k, 0, S, f"term{(3 * t + k) % TERM_SLOTS}")
+                for b in range(4):
                     nc.tensor.matmul(
-                        at_ps[:, t, :], term[:], ident[:], start=(k == 0), stop=(k == 2), is_transpose=True
+                        at_ps[b][:], term[:, b * P : (b + 1) * P], ident[:],
+                        start=(k == 0), stop=(k == 2), is_transpose=True,
                     )
-            at_sb = ring.tile([P, planes, P], F32, name="at_sb")
-            nc.scalar.copy(at_sb[:], at_ps[:])
-            a_ps = bank(6 + c % 2, [P, planes, CH])
-            for t in range(planes):
-                nc.tensor.transpose(a_ps[:, t, :], at_sb[:, t, :], ident[:])
-            sq = ring.tile([P, planes, CH], F32, name="sq")
+            at_sb = keep.tile([P, 4, P], F32, name="at_sb", tag="w2_raw" if t == 0 else f"at_sb{t}")
+            a_ps = bank(6 + t % 2, [P, S])
+            for b in range(4):
+                nc.scalar.copy(at_sb[:, b, :], at_ps[b][:])
+            for b in range(4):
+                nc.tensor.transpose(a_ps[:, b * P : (b + 1) * P], at_sb[:, b, :], ident[:])
+            sq = ring.tile([P, S], F32, name="sq")
             nc.scalar.activation(sq[:], a_ps[:], SQUARE)
-            for t in range(planes):
-                nc.scalar.activation(zz[:, t, 0:CH], a_ps[:, t, :], COPY, scale=c1_t[:, t : t + 1])
-            for t in range(planes):
-                nc.scalar.activation(zz[:, t, CH : 2 * CH], sq[:, t, :], COPY, scale=c2_t[:, t : t + 1])
+            nc.scalar.activation(zz[:, t, 0, :], a_ps[:], COPY, scale=c1_t[:, t : t + 1])
+            nc.scalar.activation(zz[:, t, 1, :], sq[:], COPY, scale=c2_t[:, t : t + 1])
 
-        def front_direct(c, zz, first):
-            part = ring.tile([P, PACK, CH], F32, name="part")
-            a_sb = ring.tile([P, PACK, CH], F32, name="a_sb")
+        def last_plane(b):
+            first, width = BLOCKS[b]
+            t = PACK - 1
+            cols = slice(first, first + width)
+            terms = [
+                gather(t, k, first, width, "zi0" if (b, k) == (2, 0) else f"term{(9 + k) % TERM_SLOTS}")
+                for k in range(3)
+            ]
+            part = keep.tile([P, width], F32, name=f"part{b}")
+            a_sb = keep.tile([P, width], F32, name=f"a_sb{b}")
+            nc.vector.tensor_tensor(part[:], terms[0][:], terms[1][:], ADD)
+            nc.vector.tensor_tensor(a_sb[:], part[:], terms[2][:], ADD)
+            nc.vector.scalar_tensor_tensor(zz[:, t, 1, cols], a_sb[:], c2_t[:, t : t + 1], a_sb[:], MULT, MULT)
+            nc.scalar.activation(zz[:, t, 0, cols], a_sb[:], COPY, scale=c1_t[:, t : t + 1])
 
-            def finish(t, term):
-                nc.vector.tensor_tensor(a_sb[:, t, :], part[:, t, :], term[:], ADD)
-                nc.scalar.activation(zz[:, t, 0:CH], a_sb[:, t, :], COPY, scale=c1_t[:, t : t + 1])
-
-            def second(t):
-                nc.vector.scalar_tensor_tensor(
-                    zz[:, t, CH : 2 * CH], a_sb[:, t, :], c2_t[:, t : t + 1], a_sb[:, t, :], MULT, MULT
+        def last_product(b):
+            first, width = BLOCKS[b]
+            final = b == len(BLOCKS) - 1
+            zi = keep.tile([P, 2, width, PACK], BF16, name="zi", tag=f"zi{b}", align_bytes=64)
+            for o in range(2):
+                copy = nc.scalar.copy if o == 0 and not final else nc.vector.tensor_copy
+                copy(
+                    zi[:, o, :, :].rearrange("p (c i) t -> p c t i", i=4),
+                    zz[:, :, o, first : first + width].rearrange("p t (c i) -> p c t i", i=4),
                 )
-
-            last = None
-            for t in range(first, PACK):
-                term0 = gather(c, t, 0)
-                if last is not None:
-                    finish(t - 1, last)
-                term1 = gather(c, t, 1)
-                if last is not None:
-                    second(t - 1)
-                last = gather(c, t, 2)
-                nc.vector.tensor_tensor(part[:, t, :], term0[:], term1[:], ADD)
-            finish(PACK - 1, last)
-            second(PACK - 1)
-
-        def back(c, zz):
-            zi = ring.tile([P, 2 * CH, PACK], BF16, name="zi", align_bytes=64)
-            dst = zi[:].rearrange("p (c i) t -> p c t i", i=4)
-            src = zz[:].rearrange("p t (c i) -> p c t i", i=4)
-            if c < 2:
-                nc.scalar.copy(dst, src)
-            else:
-                nc.vector.tensor_copy(dst, src)
-            zq = ring.tile([P, 2 * CH], U32, name="zq", align_bytes=64)
-            zs = ring.tile([P, 2 * CH], U8, name="zs", align_bytes=64)
-            nc.vector.quantize_mx(out=zq[:].bitcast(FP8X4), scales=zs[:], in_=zi[:].rearrange("p j t -> p (j t)"))
+            zq = keep.tile([P, 2 * width], U32, name=f"zq{b}", align_bytes=64)
+            zs = keep.tile([P, 2 * width], U8, name=f"zs{b}", align_bytes=64)
+            nc.vector.quantize_mx(out=zq[:].bitcast(FP8X4), scales=zs[:], in_=zi[:].rearrange("p o j t -> p (o j t)"))
             for half in range(2):
-                o_ps = bank(2 * (c % 2) + half, [P, 2, CH])
+                o_ps = bank(2 * b + half, [P, 2, width])
                 for a in range(2):
                     rows = slice((2 * half + a) * P, (2 * half + a + 1) * P)
                     for i in range(2):
@@ -212,25 +213,23 @@ def tile_picked_ace8_none_p_kernel(
                             out=o_ps[:, a, :],
                             lhsT=w_q[i][:, rows].bitcast(FP8X4),
                             lhsT_scale=w_s[i][:, rows],
-                            rhs=zq[:, i * CH : (i + 1) * CH].bitcast(FP8X4),
-                            rhs_scale=zs[:, i * CH : (i + 1) * CH],
+                            rhs=zq[:, i * width : (i + 1) * width].bitcast(FP8X4),
+                            rhs_scale=zs[:, i * width : (i + 1) * width],
                             start=(i == 0),
                             stop=(i == 1),
                         )
-                o_sb = ring.tile([P, 2, CH], F32, name="o_sb", tag=f"o_sb{half}")
-                if c == CHUNKS - 1 and half == 1:
-                    nc.vector.tensor_copy(o_sb[:], o_ps[:])
-                else:
-                    nc.scalar.copy(o_sb[:], o_ps[:])
-                nc.sync.dma_start(out_v[:, 2 * half : 2 * half + 2, c * CH : (c + 1) * CH], o_sb[:])
+                o_sb = keep.tile([P, 2, width], F32, name=f"o_sb{b}_{half}")
+                copy = nc.vector.tensor_copy if final and half == 1 else nc.scalar.copy
+                copy(o_sb[:], o_ps[:])
+                nc.sync.dma_start(out_v[:, 2 * half : 2 * half + 2, first : first + width], o_sb[:])
 
-        zz = [keep.tile([P, PACK, 2 * CH], BF16, name=f"zz{c}") for c in range(CHUNKS)]
-        front_pe(0, zz[0], PACK)
-        front_pe(1, zz[1], PACK)
-        back(0, zz[0])
-        front_pe(2, zz[2], PACK)
-        back(1, zz[1])
-        front_pe(3, zz[3], 2)
-        back(2, zz[2])
-        front_direct(3, zz[3], 2)
-        back(3, zz[3])
+        last_weights(0)
+        for t in range(PACK - 1):
+            plane_by_transposes(t)
+        last_weights(1)
+        last_plane(0)
+        last_plane(1)
+        last_product(0)
+        last_plane(2)
+        last_product(1)
+        last_product(2)

@@ -21,8 +21,11 @@ SQUARE = mybir.ActivationFunctionType.Square
 P = 128
 PACK = 4
 HALF = S // 2
-TERM_SLOTS = 4
-BLOCKS = ((0, 128), (128, 256), (384, 128))
+ABS = mybir.ActivationFunctionType.Abs
+SIGN = mybir.ActivationFunctionType.Sign
+SQRT = mybir.ActivationFunctionType.Sqrt
+TERM_SLOTS = 27
+TINY = 2.0**-120
 
 
 def tile_picked_ace8_none_p_kernel(
@@ -31,7 +34,6 @@ def tile_picked_ace8_none_p_kernel(
     nc = tc.nc
     with ExitStack() as ctx:
         keep = ctx.enter_context(tc.tile_pool(name="keep", bufs=1))
-        ring = ctx.enter_context(tc.tile_pool(name="ring", bufs=2))
         psum = ctx.enter_context(tc.psum_pool(name="psum", bufs=1))
 
         def bank(b, shape):
@@ -43,7 +45,7 @@ def tile_picked_ace8_none_p_kernel(
             return lt
 
         def load_gain(name, src):
-            gt = keep.tile([P, S], F32, name=name)
+            gt = keep.tile([P, S], F32, name=name, tag=name, align_bytes=64)
             nc.sync.dma_start(gt[:], src)
             return gt
 
@@ -52,42 +54,52 @@ def tile_picked_ace8_none_p_kernel(
             nc.sync.dma_start(wr[:], src.rearrange("(p j) c -> p j c", j=PACK))
             return wr
 
+        def load_factor(name, src):
+            ct = keep.tile([P, PACK], F32, name=name)
+            nc.sync.dma_start(ct[:], src.rearrange("(p t) o -> p (t o)", t=PACK))
+            return ct
+
         xs = keep.tile([P, T], U8, name="xs", align_bytes=64)
-        nc.gpsimd.memset(xs[:].bitcast(I32), 0)
+        nc.gpsimd.memset(xs[:, 0:640].bitcast(I32), 0)
+        nc.vector.memset(xs[:, 640:T].bitcast(I32), 0)
         offs_t = load_list("offs_t", offs)
-        lists = [load_list("list0", p1), load_list("list1", p2)]
+        c2_t = load_factor("c2_t", c2)
         xw = keep.tile([P, T], I32, name="xw", align_bytes=64)
         nc.sync.dma_start(xw[:], x_words[0].rearrange("p n t -> p (n t)").bitcast(I32))
-        lists.append(load_list("list2", p3))
-        c1_t = keep.tile([P, PACK], F32, name="c1_t")
-        nc.sync.dma_start(c1_t[:], c1.rearrange("(p t) o -> p (t o)", t=PACK))
         for q in range(4):
             nc.sync.dma_start(
                 xs[32 * q : 32 * q + 4, :].bitcast(I32), x_scales[0, 4 * q : 4 * q + 4, :].bitcast(I32)
             )
         w1_raw = load_rows("w1_raw", w1)
-        gains = [load_gain("gain0", g1), load_gain("gain1", g2), load_gain("gain2", g3)]
-        c2_t = keep.tile([P, PACK], F32, name="c2_t")
-        nc.sync.dma_start(c2_t[:], c2.rearrange("(p t) o -> p (t o)", t=PACK))
-        w_raw = [load_rows("w2_raw", w2), load_rows("w3_raw", w3)]
+        lists, gains = [], []
+        for k, (pk, gk) in enumerate(((p1, g1), (p2, g2), (p3, g3))):
+            lists.append(load_list(f"list{k}", pk))
+            gains.append(load_gain(f"gain{k}", gk))
+        w_raw = [load_rows("w2_raw", w2)]
+        c1_t = load_factor("c1_t", c1)
+        w_raw.append(load_rows("w3_raw", w3))
 
         ident = keep.tile([P, P], F32, name="ident")
         make_identity(nc, ident[:])
 
-        y = [keep.tile([P, 2 * S if t < PACK - 1 else S], F32, name=f"y{t}") for t in range(PACK)]
-        for t in range(PACK - 1):
-            nc.gpsimd.memset(y[t][:, S : 2 * S], 0.0)
+        def small(name):
+            return keep.tile([P, PACK], F32, name=name)
 
-        xw_g = keep.tile([P, S], U32, name="xw_g", align_bytes=64)
-        nc.vector.tensor_copy(xw_g[:], xw[:].bitcast(U32).indirect(offs_t[:]))
-        xs_g = keep.tile([P, S], U8, name="xs_g", align_bytes=64)
-        nc.vector.tensor_copy(xs_g[:], xs[:].indirect(offs_t[:]))
+        mag, root, sign, inv_root, ratio = (small(n) for n in ("mag", "root", "sign", "inv_root", "ratio"))
+        nc.scalar.activation(mag[:], c2_t[:], ABS)
+        nc.scalar.activation(root[:], mag[:], SQRT, bias=TINY)
+        nc.scalar.activation(sign[:], c2_t[:], SIGN, bias=TINY)
+        nc.vector.reciprocal(inv_root[:], root[:])
 
         w1_b = keep.tile([P, PACK, P, PACK], BF16, name="w1_b", align_bytes=64)
         w1_q = keep.tile([P, H], U32, name="w1_q", align_bytes=64)
         w1_s = keep.tile([P, H], U8, name="w1_s", align_bytes=64)
         src = w1_raw[:].rearrange("p j (m t) -> p m t j", t=PACK)
         dst = w1_b[:].rearrange("p t m j -> p m t j")
+        xw_g = keep.tile([P, S], U32, name="xw_g", align_bytes=64)
+        nc.vector.tensor_copy(xw_g[:], xw[:].bitcast(U32).indirect(offs_t[:]))
+        xs_g = keep.tile([P, S], U8, name="xs_g", align_bytes=64)
+        nc.vector.tensor_copy(xs_g[:], xs[:].indirect(offs_t[:]))
 
         def quantize_w1(first, count):
             cols = slice(first * P, (first + count) * P)
@@ -97,10 +109,9 @@ def tile_picked_ace8_none_p_kernel(
                 in_=w1_b[:, first : first + count].rearrange("p t m j -> p (t m j)"),
             )
 
-        nc.vector.tensor_copy(dst[:, :, 0, :], src[:, :, 0, :])
-        nc.scalar.copy(dst[:, :, 1, :], src[:, :, 1, :])
+        nc.vector.tensor_copy(dst[:, :, 0:2, :], src[:, :, 0:2, :])
+        nc.scalar.copy(dst[:, :, 2:4, :], src[:, :, 2:4, :])
         quantize_w1(0, 1)
-        nc.vector.tensor_copy(dst[:, :, 2:4, :], src[:, :, 2:4, :])
         quantize_w1(1, 1)
         quantize_w1(2, 2)
 
@@ -115,97 +126,77 @@ def tile_picked_ace8_none_p_kernel(
                 stop=True,
             )
 
-        for h, copy in enumerate((nc.scalar.copy, nc.vector.tensor_copy)):
+        y = [keep.tile([P, S], F32, name=f"y{t}", tag=f"y{t}", align_bytes=64) for t in range(PACK)]
+        for h in range(2):
             cols = slice(h * HALF, (h + 1) * HALF)
             ps = bank(h, [P, HALF])
             first_product(ps[:], 0, cols)
-            copy(y[0][:, cols], ps[:])
+            if h == 0:
+                nc.scalar.activation(y[0][:, cols], ps[:], COPY, scale=root[:, 0:1])
+            else:
+                nc.vector.tensor_scalar(y[0][:, cols], ps[:], root[:, 0:1], None, MULT)
         for t in range(1, PACK):
-            ps = bank((6, 7, 0)[t - 1], [P, S])
+            ps = bank((6, 7, 2)[t - 1], [P, S])
             first_product(ps[:], t, slice(0, S))
-            nc.scalar.copy(y[t][:, 0:S], ps[:])
+            nc.scalar.activation(y[t][:], ps[:], COPY, scale=root[:, t : t + 1])
+        nc.gpsimd.tensor_tensor(ratio[:], c1_t[:], inv_root[:], MULT)
 
-        w_q, w_s = [], []
+        w_b = [keep.tile([P, N, PACK], BF16, name=f"w_b{i}", align_bytes=64) for i in range(2)]
+        w_q = []
+        w_s = [keep.tile([P, N], U8, name=f"w_s{i}", align_bytes=64) for i in range(2)]
+        w3_signed = keep.tile([P, PACK, N], BF16, name="w3_signed")
 
-        def last_weights(i):
-            wb = keep.tile([P, N, PACK], BF16, name=f"w_b{i}", align_bytes=64)
-            for h in range(4):
-                cols = slice(h * P, (h + 1) * P)
-                nc.scalar.copy(
-                    wb[:, cols, :].rearrange("p (c i) t -> p c t i", i=4),
-                    w_raw[i][:, :, cols].rearrange("p t (c i) -> p c t i", i=4),
-                )
-            wq = keep.tile([P, N], U32, name=f"w_q{i}", align_bytes=64)
-            ws = keep.tile([P, N], U8, name=f"w_s{i}", align_bytes=64)
-            nc.vector.quantize_mx(
-                out=wq[:].bitcast(FP8X4), scales=ws[:], in_=wb[:].rearrange("p m t -> p (m t)")
+        def weave_weights(i, rows, h, copy):
+            cols = slice(h * P, (h + 1) * P)
+            copy(
+                w_b[i][:, cols, :].rearrange("p (c i) t -> p c t i", i=4),
+                rows[:, :, cols].rearrange("p t (c i) -> p c t i", i=4),
             )
-            w_q.append(wq)
-            w_s.append(ws)
+
+        def quantize_weights(i, tag):
+            w_q.append(keep.tile([P, N], U32, name=f"w_q{i}", tag=tag, align_bytes=64))
+            nc.vector.quantize_mx(
+                out=w_q[i][:].bitcast(FP8X4), scales=w_s[i][:], in_=w_b[i][:].rearrange("p m t -> p (m t)")
+            )
 
         out_v = out.rearrange("(a p) j -> p a j", p=P)
-        zz = keep.tile([P, PACK, 2, S], BF16, name="zz")
 
-        def gather(t, k, first, width, tag):
-            term = keep.tile([P, width], F32, name="term", tag=tag, align_bytes=64)
-            nc.vector.tensor_tensor(
-                term[:],
-                y[t][:].indirect(lists[k][:, first // 16 : (first + width) // 16]),
-                gains[k][:, first : first + width],
-                MULT,
-            )
-            return term
+        turn = []
 
-        def plane_by_transposes(t):
-            at_ps = [bank(2 + b, [P, P]) for b in range(4)]
+        def sum_plane(t, first, blocks):
+            lo, width = first * P, blocks * P
+            at_ps = [bank(6 * (len(turn) // 3 % 2) + b, [P, P]) for b in range(blocks)]
             for k in range(3):
-                term = gather(t, k, 0, S, f"term{(3 * t + k) % TERM_SLOTS}")
-                for b in range(4):
+                term = keep.tile([P, width], F32, name="term", tag=f"term{len(turn) % TERM_SLOTS}", align_bytes=64)
+                turn.append(k)
+                nc.vector.tensor_tensor(
+                    term[:], y[t][:].indirect(lists[k][:, lo // 16 : (lo + width) // 16]), gains[k][:, lo : lo + width], MULT
+                )
+                for b in range(blocks):
                     nc.tensor.matmul(
                         at_ps[b][:], term[:, b * P : (b + 1) * P], ident[:],
                         start=(k == 0), stop=(k == 2), is_transpose=True,
                     )
-            at_sb = keep.tile([P, 4, P], F32, name="at_sb", tag="w2_raw" if t == 0 else f"at_sb{t}")
-            a_ps = bank(6 + t % 2, [P, S])
-            for b in range(4):
+            at_sb = keep.tile([P, blocks, P], F32, name="at_sb", tag=f"at_sb{len(turn) // 3 % 2}")
+            for b in range(blocks):
                 nc.scalar.copy(at_sb[:, b, :], at_ps[b][:])
-            for b in range(4):
-                nc.tensor.transpose(a_ps[:, b * P : (b + 1) * P], at_sb[:, b, :], ident[:])
-            sq = ring.tile([P, S], F32, name="sq")
-            nc.scalar.activation(sq[:], a_ps[:], SQUARE)
-            nc.scalar.activation(zz[:, t, 0, :], a_ps[:], COPY, scale=c1_t[:, t : t + 1])
-            nc.scalar.activation(zz[:, t, 1, :], sq[:], COPY, scale=c2_t[:, t : t + 1])
+            for b in range(blocks):
+                nc.tensor.transpose(a_blk[first + b][:, t, :], at_sb[:, b, :], ident[:])
 
-        def last_plane(b):
-            first, width = BLOCKS[b]
-            t = PACK - 1
-            cols = slice(first, first + width)
-            terms = [
-                gather(t, k, first, width, "zi0" if (b, k) == (2, 0) else f"term{(9 + k) % TERM_SLOTS}")
-                for k in range(3)
-            ]
-            part = keep.tile([P, width], F32, name=f"part{b}")
-            a_sb = keep.tile([P, width], F32, name=f"a_sb{b}")
-            nc.vector.tensor_tensor(part[:], terms[0][:], terms[1][:], ADD)
-            nc.vector.tensor_tensor(a_sb[:], part[:], terms[2][:], ADD)
-            nc.vector.scalar_tensor_tensor(zz[:, t, 1, cols], a_sb[:], c2_t[:, t : t + 1], a_sb[:], MULT, MULT)
-            nc.scalar.activation(zz[:, t, 0, cols], a_sb[:], COPY, scale=c1_t[:, t : t + 1])
+        def first_order(zi, a_ps):
+            nc.vector.tensor_tensor(
+                zi, a_ps[:].rearrange("p t j -> p j t"), ratio[:].unsqueeze(1).to_broadcast([P, P, PACK]), MULT
+            )
 
-        def last_product(b):
-            first, width = BLOCKS[b]
-            final = b == len(BLOCKS) - 1
-            zi = keep.tile([P, 2, width, PACK], BF16, name="zi", tag=f"zi{b}", align_bytes=64)
-            for o in range(2):
-                copy = nc.scalar.copy if o == 0 and not final else nc.vector.tensor_copy
-                copy(
-                    zi[:, o, :, :].rearrange("p (c i) t -> p c t i", i=4),
-                    zz[:, :, o, first : first + width].rearrange("p t (c i) -> p c t i", i=4),
-                )
-            zq = keep.tile([P, 2 * width], U32, name=f"zq{b}", align_bytes=64)
-            zs = keep.tile([P, 2 * width], U8, name=f"zs{b}", align_bytes=64)
+        def second_order(zi, a_ps):
+            nc.scalar.activation(zi, a_ps[:].rearrange("p t j -> p j t"), SQUARE)
+
+        def last_product(name, zi, first, width, banks, copies):
+            zq = keep.tile([P, 2 * width], U32, name=f"zq{name}", tag="term26" if name == "a" else f"zq{name}", align_bytes=64)
+            zs = keep.tile([P, 2 * width], U8, name=f"zs{name}", align_bytes=64)
             nc.vector.quantize_mx(out=zq[:].bitcast(FP8X4), scales=zs[:], in_=zi[:].rearrange("p o j t -> p (o j t)"))
             for half in range(2):
-                o_ps = bank(2 * b + half, [P, 2, width])
+                o_ps = bank(banks[half], [P, 2, width])
                 for a in range(2):
                     rows = slice((2 * half + a) * P, (2 * half + a + 1) * P)
                     for i in range(2):
@@ -218,18 +209,62 @@ def tile_picked_ace8_none_p_kernel(
                             start=(i == 0),
                             stop=(i == 1),
                         )
-                o_sb = keep.tile([P, 2, width], F32, name=f"o_sb{b}_{half}")
-                copy = nc.vector.tensor_copy if final and half == 1 else nc.scalar.copy
-                copy(o_sb[:], o_ps[:])
+                o_sb = keep.tile([P, 2, width], F32, name=f"o_sb{name}_{half}")
+                copies[half](o_sb[:], o_ps[:])
                 nc.sync.dma_start(out_v[:, 2 * half : 2 * half + 2, first : first + width], o_sb[:])
 
-        last_weights(0)
-        for t in range(PACK - 1):
-            plane_by_transposes(t)
-        last_weights(1)
-        last_plane(0)
-        last_plane(1)
-        last_product(0)
-        last_plane(2)
-        last_product(1)
-        last_product(2)
+        a_blk = [bank(2 + b, [P, PACK, P]) for b in range(4)]
+        zi_a = keep.tile([P, 2, HALF, PACK], BF16, name="zi_a", align_bytes=64)
+        z2_rows = [keep.tile([P, PACK, P], BF16, name=f"z2_rows{b}") for b in range(2)]
+
+        def sign_rows(t):
+            nc.scalar.activation(w3_signed[:, t, :], w_raw[1][:, t, :], COPY, scale=sign[:, t : t + 1])
+
+        def z2_plane(b, t):
+            nc.scalar.activation(z2_rows[b][:, t, :], a_blk[b][:, t, :], COPY, scale=ratio[:, t : t + 1])
+
+        def z2_weave(b):
+            nc.scalar.copy(
+                zi_a[:, 0, b * P : (b + 1) * P, :].rearrange("p (c i) t -> p c t i", i=4),
+                z2_rows[b][:].rearrange("p t (c i) -> p c t i", i=4),
+            )
+
+        weave_weights(0, w_raw[0], 0, nc.scalar.copy)
+        sum_plane(0, 0, 2)
+        weave_weights(0, w_raw[0], 1, nc.scalar.copy)
+        weave_weights(0, w_raw[0], 2, nc.scalar.copy)
+        sum_plane(1, 0, 2)
+        z2_plane(0, 0)
+        weave_weights(0, w_raw[0], 3, nc.scalar.copy)
+        quantize_weights(0, "w_q0")
+        sign_rows(0)
+        sum_plane(2, 0, 2)
+        z2_plane(0, 1)
+        sign_rows(1)
+        sign_rows(2)
+        sum_plane(3, 0, 2)
+        z2_plane(0, 2)
+        sign_rows(3)
+        weave_weights(1, w3_signed, 0, nc.scalar.copy)
+        sum_plane(0, 2, 2)
+        z2_plane(0, 3)
+        second_order(zi_a[:, 1, 1 * P : 2 * P, :], a_blk[1])
+        second_order(zi_a[:, 1, 0 * P : 1 * P, :], a_blk[0])
+        first_order(zi_a[:, 0, 1 * P : 2 * P, :], a_blk[1])
+        sum_plane(1, 2, 2)
+        z2_weave(0)
+        weave_weights(1, w3_signed, 1, nc.scalar.copy)
+        sum_plane(2, 2, 2)
+        weave_weights(1, w3_signed, 2, nc.scalar.copy)
+        weave_weights(1, w3_signed, 3, nc.scalar.copy)
+        sum_plane(3, 2, 1)
+        sum_plane(3, 3, 1)
+        quantize_weights(1, "y3")
+        last_product("a", zi_a, 0, HALF, (0, 6), (nc.scalar.copy, nc.scalar.copy))
+        zi_b = [keep.tile([P, 2, P, PACK], BF16, name=f"zi_b{b}", align_bytes=64) for b in range(2)]
+        for b in range(2):
+            second_order(zi_b[b][:, 1], a_blk[2 + b])
+        for b in range(2):
+            first_order(zi_b[b][:, 0], a_blk[2 + b])
+        last_product("b0", zi_b[0], HALF, P, (1, 7), (nc.scalar.copy, nc.vector.tensor_copy))
+        last_product("b1", zi_b[1], HALF + P, P, (2, 3), (nc.scalar.copy, nc.vector.tensor_copy))

@@ -139,7 +139,7 @@ def tile_picked_ace8_none_p_kernel(
             ps = bank((6, 7, 2)[t - 1], [P, S])
             first_product(ps[:], t, slice(0, S))
             nc.scalar.activation(y[t][:], ps[:], COPY, scale=root[:, t : t + 1])
-        nc.gpsimd.tensor_tensor(ratio[:], c1_t[:], inv_root[:], MULT)
+        nc.vector.tensor_tensor(ratio[:], c1_t[:], inv_root[:], MULT)
 
         w_b = [keep.tile([P, N, PACK], BF16, name=f"w_b{i}", align_bytes=64) for i in range(2)]
         w_q = []

@@ -139,7 +139,8 @@ def tile_picked_ace8_none_p_kernel(
             ps = bank((6, 7, 2)[t - 1], [P, S])
             first_product(ps[:], t, slice(0, S))
             nc.scalar.activation(y[t][:], ps[:], COPY, scale=root[:, t : t + 1])
-        nc.vector.tensor_tensor(ratio[:], c1_t[:], inv_root[:], MULT)
+        for t in range(PACK):
+            nc.scalar.activation(ratio[:, t : t + 1], c1_t[:, t : t + 1], COPY, scale=inv_root[:, t : t + 1])
 
         w_b = [keep.tile([P, N, PACK], BF16, name=f"w_b{i}", align_bytes=64) for i in range(2)]
         w_q = []

@@ -182,15 +182,15 @@ def tile_picked_ace8_none_p_kernel(
             for b in range(blocks):
                 nc.scalar.copy(at_sb[:, b, :], at_ps[b][:])
             for b in range(blocks):
-                nc.tensor.transpose(a_blk[first + b][:, t, :], at_sb[:, b, :], ident[:])
+                nc.tensor.transpose(a_blk[first + b][:, :, t], at_sb[:, b, :], ident[:])
 
         def first_order(zi, a_ps):
             nc.vector.tensor_tensor(
-                zi, a_ps[:].rearrange("p t j -> p j t"), ratio[:].unsqueeze(1).to_broadcast([P, P, PACK]), MULT
+                zi, a_ps[:], ratio[:].unsqueeze(1).to_broadcast([P, P, PACK]), MULT
             )
 
         def second_order(zi, a_ps):
-            nc.scalar.activation(zi, a_ps[:].rearrange("p t j -> p j t"), SQUARE)
+            nc.scalar.activation(zi, a_ps[:], SQUARE)
 
         def last_product(name, zi, first, width, banks, copies):
             zq = keep.tile([P, 2 * width], U32, name=f"zq{name}", tag="term26" if name == "a" else f"zq{name}", align_bytes=64)
@@ -214,7 +214,7 @@ def tile_picked_ace8_none_p_kernel(
                 copies[half](o_sb[:], o_ps[:])
                 nc.sync.dma_start(out_v[:, 2 * half : 2 * half + 2, first : first + width], o_sb[:])
 
-        a_blk = [bank(2 + b, [P, PACK, P]) for b in range(4)]
+        a_blk = [bank(2 + b, [P, P, PACK]) for b in range(4)]
         zi_a = keep.tile([P, 2, HALF, PACK], BF16, name="zi_a", align_bytes=64)
         z2_rows = [keep.tile([P, PACK, P], BF16, name=f"z2_rows{b}") for b in range(2)]
 
@@ -222,7 +222,7 @@ def tile_picked_ace8_none_p_kernel(
             nc.scalar.activation(w3_signed[:, t, :], w_raw[1][:, t, :], COPY, scale=sign[:, t : t + 1])
 
         def z2_plane(b, t):
-            nc.scalar.activation(z2_rows[b][:, t, :], a_blk[b][:, t, :], COPY, scale=ratio[:, t : t + 1])
+            nc.scalar.activation(z2_rows[b][:, t, :], a_blk[b][:, :, t], COPY, scale=ratio[:, t : t + 1])
 
         def z2_weave(b):
             nc.scalar.copy(

@@ -14,18 +14,22 @@ U16 = mybir.dt.uint16
 U8 = mybir.dt.uint8
 FP8X4 = mybir.dt.float8_e4m3fn_x4
 MULT = mybir.AluOpType.mult
-ADD = mybir.AluOpType.add
 COPY = mybir.ActivationFunctionType.Copy
 SQUARE = mybir.ActivationFunctionType.Square
+ABS = mybir.ActivationFunctionType.Abs
+SIGN = mybir.ActivationFunctionType.Sign
+SQRT = mybir.ActivationFunctionType.Sqrt
 
 P = 128
 PACK = 4
 HALF = S // 2
-ABS = mybir.ActivationFunctionType.Abs
-SIGN = mybir.ActivationFunctionType.Sign
-SQRT = mybir.ActivationFunctionType.Sqrt
-TERM_SLOTS = 27
+LIST_ROWS = 16
+TERMS = 3
 TINY = 2.0**-120
+GPSIMD_CLEARS = 640
+JOBS_PER_UNIT = 2
+ADD_BANKS = ((0, 1), (6, 7))
+SUM_BANKS = (2, 3, 4, 5)
 
 
 def tile_picked_ace8_none_p_kernel(
@@ -40,7 +44,7 @@ def tile_picked_ace8_none_p_kernel(
             return psum.tile(shape, F32, name=f"bank{b}", tag=f"bank{b}")
 
         def load_list(name, src):
-            lt = keep.tile([P, S // 16], U16, name=name)
+            lt = keep.tile([P, S // LIST_ROWS], U16, name=name)
             nc.sync.dma_start(lt[:], src)
             return lt
 
@@ -60,8 +64,8 @@ def tile_picked_ace8_none_p_kernel(
             return ct
 
         xs = keep.tile([P, T], U8, name="xs", align_bytes=64)
-        nc.gpsimd.memset(xs[:, 0:640].bitcast(I32), 0)
-        nc.vector.memset(xs[:, 640:T].bitcast(I32), 0)
+        nc.gpsimd.memset(xs[:, 0:GPSIMD_CLEARS].bitcast(I32), 0)
+        nc.vector.memset(xs[:, GPSIMD_CLEARS:T].bitcast(I32), 0)
         offs_t = load_list("offs_t", offs)
         c2_t = load_factor("c2_t", c2)
         xw = keep.tile([P, T], I32, name="xw", align_bytes=64)
@@ -72,20 +76,19 @@ def tile_picked_ace8_none_p_kernel(
             )
         w1_raw = load_rows("w1_raw", w1)
         lists, gains = [], []
-        for k, (pk, gk) in enumerate(((p1, g1), (p2, g2), (p3, g3))):
-            lists.append(load_list(f"list{k}", pk))
-            gains.append(load_gain(f"gain{k}", gk))
-        w_raw = [load_rows("w2_raw", w2)]
+        for k, (list_k, gain_k) in enumerate(((p1, g1), (p2, g2), (p3, g3))):
+            lists.append(load_list(f"list{k}", list_k))
+            gains.append(load_gain(f"gain{k}", gain_k))
+        w2_raw = load_rows("w2_raw", w2)
         c1_t = load_factor("c1_t", c1)
-        w_raw.append(load_rows("w3_raw", w3))
+        w3_raw = load_rows("w3_raw", w3)
 
         ident = keep.tile([P, P], F32, name="ident")
         make_identity(nc, ident[:])
 
-        def small(name):
-            return keep.tile([P, PACK], F32, name=name)
-
-        mag, root, sign, inv_root, ratio = (small(n) for n in ("mag", "root", "sign", "inv_root", "ratio"))
+        mag, root, sign, inv_root, ratio = (
+            keep.tile([P, PACK], F32, name=name) for name in ("mag", "root", "sign", "inv_root", "ratio")
+        )
         nc.scalar.activation(mag[:], c2_t[:], ABS)
         nc.scalar.activation(root[:], mag[:], SQRT, bias=TINY)
         nc.scalar.activation(sign[:], c2_t[:], SIGN, bias=TINY)
@@ -94,8 +97,8 @@ def tile_picked_ace8_none_p_kernel(
         w1_b = keep.tile([P, PACK, P, PACK], BF16, name="w1_b", align_bytes=64)
         w1_q = keep.tile([P, H], U32, name="w1_q", align_bytes=64)
         w1_s = keep.tile([P, H], U8, name="w1_s", align_bytes=64)
-        src = w1_raw[:].rearrange("p j (m t) -> p m t j", t=PACK)
-        dst = w1_b[:].rearrange("p t m j -> p m t j")
+        w1_from = w1_raw[:].rearrange("p j (m t) -> p m t j", t=PACK)
+        w1_to = w1_b[:].rearrange("p t m j -> p m t j")
         xw_g = keep.tile([P, S], U32, name="xw_g", align_bytes=64)
         nc.vector.tensor_copy(xw_g[:], xw[:].bitcast(U32).indirect(offs_t[:]))
         xs_g = keep.tile([P, S], U8, name="xs_g", align_bytes=64)
@@ -109,8 +112,8 @@ def tile_picked_ace8_none_p_kernel(
                 in_=w1_b[:, first : first + count].rearrange("p t m j -> p (t m j)"),
             )
 
-        nc.vector.tensor_copy(dst[:, :, 0:2, :], src[:, :, 0:2, :])
-        nc.scalar.copy(dst[:, :, 2:4, :], src[:, :, 2:4, :])
+        nc.vector.tensor_copy(w1_to[:, :, 0:2, :], w1_from[:, :, 0:2, :])
+        nc.scalar.copy(w1_to[:, :, 2:4, :], w1_from[:, :, 2:4, :])
         quantize_w1(0, 1)
         quantize_w1(1, 1)
         quantize_w1(2, 2)
@@ -127,16 +130,14 @@ def tile_picked_ace8_none_p_kernel(
             )
 
         y = [keep.tile([P, S], F32, name=f"y{t}", tag=f"y{t}", align_bytes=64) for t in range(PACK)]
-        for h in range(2):
-            cols = slice(h * HALF, (h + 1) * HALF)
-            ps = bank(h, [P, HALF])
-            first_product(ps[:], 0, cols)
-            if h == 0:
-                nc.scalar.activation(y[0][:, cols], ps[:], COPY, scale=root[:, 0:1])
-            else:
-                nc.vector.tensor_scalar(y[0][:, cols], ps[:], root[:, 0:1], None, MULT)
-        for t in range(1, PACK):
-            ps = bank((6, 7, 2)[t - 1], [P, S])
+        ps = bank(0, [P, HALF])
+        first_product(ps[:], 0, slice(0, HALF))
+        nc.scalar.activation(y[0][:, 0:HALF], ps[:], COPY, scale=root[:, 0:1])
+        ps = bank(1, [P, HALF])
+        first_product(ps[:], 0, slice(HALF, S))
+        nc.vector.tensor_scalar(y[0][:, HALF:S], ps[:], root[:, 0:1], None, MULT)
+        for t, b in zip(range(1, PACK), ADD_BANKS[1] + SUM_BANKS[:1]):
+            ps = bank(b, [P, S])
             first_product(ps[:], t, slice(0, S))
             nc.scalar.activation(y[t][:], ps[:], COPY, scale=root[:, t : t + 1])
         for t in range(PACK):
@@ -147,12 +148,17 @@ def tile_picked_ace8_none_p_kernel(
         w_s = [keep.tile([P, N], U8, name=f"w_s{i}", align_bytes=64) for i in range(2)]
         w3_signed = keep.tile([P, PACK, N], BF16, name="w3_signed")
 
-        def weave_weights(i, rows, h, copy):
-            cols = slice(h * P, (h + 1) * P)
-            copy(
-                w_b[i][:, cols, :].rearrange("p (c i) t -> p c t i", i=4),
-                rows[:, :, cols].rearrange("p t (c i) -> p c t i", i=4),
+        def weave(dst, rows):
+            nc.scalar.copy(
+                dst.rearrange("p (c i) t -> p c t i", i=4), rows.rearrange("p t (c i) -> p c t i", i=4)
             )
+
+        def weave_weights(i, rows, quarter):
+            cols = slice(quarter * P, (quarter + 1) * P)
+            weave(w_b[i][:, cols, :], rows[:, :, cols])
+
+        def sign_rows(t):
+            nc.scalar.activation(w3_signed[:, t, :], w3_raw[:, t, :], COPY, scale=sign[:, t : t + 1])
 
         def quantize_weights(i, tag):
             w_q.append(keep.tile([P, N], U32, name=f"w_q{i}", tag=tag, align_bytes=64))
@@ -160,46 +166,53 @@ def tile_picked_ace8_none_p_kernel(
                 out=w_q[i][:].bitcast(FP8X4), scales=w_s[i][:], in_=w_b[i][:].rearrange("p m t -> p (m t)")
             )
 
+        units = [(t, first, 2) for first in (0, 2) for t in range(PACK)]
+        units = units[:-1] + [(PACK - 1, 2, 1), (PACK - 1, 3, 1)]
+        last_term_tag = f"term{TERMS * len(units) - 1}"
         out_v = out.rearrange("(a p) j -> p a j", p=P)
 
-        turn = []
-
-        def sum_plane(t, first, blocks):
+        def sum_unit(u):
+            t, first, blocks = units[u]
             lo, width = first * P, blocks * P
-            at_ps = [bank(6 * (len(turn) // 3 % 2) + b, [P, P]) for b in range(blocks)]
-            for k in range(3):
-                term = keep.tile([P, width], F32, name="term", tag=f"term{len(turn) % TERM_SLOTS}", align_bytes=64)
-                turn.append(k)
+            turned_ps = [bank(ADD_BANKS[u % 2][b], [P, P]) for b in range(blocks)]
+            for k in range(TERMS):
+                term = keep.tile([P, width], F32, name="term", tag=f"term{TERMS * u + k}", align_bytes=64)
                 nc.vector.tensor_tensor(
-                    term[:], y[t][:].indirect(lists[k][:, lo // 16 : (lo + width) // 16]), gains[k][:, lo : lo + width], MULT
+                    term[:],
+                    y[t][:].indirect(lists[k][:, lo // LIST_ROWS : (lo + width) // LIST_ROWS]),
+                    gains[k][:, lo : lo + width],
+                    MULT,
                 )
                 for b in range(blocks):
                     nc.tensor.matmul(
-                        at_ps[b][:], term[:, b * P : (b + 1) * P], ident[:],
-                        start=(k == 0), stop=(k == 2), is_transpose=True,
+                        turned_ps[b][:], term[:, b * P : (b + 1) * P], ident[:],
+                        start=(k == 0), stop=(k == TERMS - 1), is_transpose=True,
                     )
-            at_sb = keep.tile([P, blocks, P], F32, name="at_sb", tag=f"at_sb{len(turn) // 3 % 2}")
+            turned = keep.tile([P, blocks, P], F32, name="turned", tag=f"turned{u % 2}")
             for b in range(blocks):
-                nc.scalar.copy(at_sb[:, b, :], at_ps[b][:])
+                nc.scalar.copy(turned[:, b, :], turned_ps[b][:])
             for b in range(blocks):
-                nc.tensor.transpose(a_blk[first + b][:, :, t], at_sb[:, b, :], ident[:])
+                nc.tensor.transpose(sums[first + b][:, :, t], turned[:, b, :], ident[:])
 
-        def first_order(zi, a_ps):
-            nc.vector.tensor_tensor(
-                zi, a_ps[:], ratio[:].unsqueeze(1).to_broadcast([P, P, PACK]), MULT
-            )
+        def first_order(dst, b):
+            nc.vector.tensor_tensor(dst, sums[b][:], ratio[:].unsqueeze(1).to_broadcast([P, P, PACK]), MULT)
 
-        def second_order(zi, a_ps):
-            nc.scalar.activation(zi, a_ps[:], SQUARE)
+        def second_order(dst, b):
+            nc.scalar.activation(dst, sums[b][:], SQUARE)
 
-        def last_product(name, zi, first, width, banks, copies):
-            zq = keep.tile([P, 2 * width], U32, name=f"zq{name}", tag="term26" if name == "a" else f"zq{name}", align_bytes=64)
+        def last_product(name, values, codes_tag, first, banks, copies):
+            width = values.shape[2]
+            zq = keep.tile([P, 2 * width], U32, name=f"zq{name}", tag=codes_tag, align_bytes=64)
             zs = keep.tile([P, 2 * width], U8, name=f"zs{name}", align_bytes=64)
-            nc.vector.quantize_mx(out=zq[:].bitcast(FP8X4), scales=zs[:], in_=zi[:].rearrange("p o j t -> p (o j t)"))
-            for half in range(2):
-                o_ps = bank(banks[half], [P, 2, width])
-                for a in range(2):
-                    rows = slice((2 * half + a) * P, (2 * half + a + 1) * P)
+            nc.vector.quantize_mx(
+                out=zq[:].bitcast(FP8X4), scales=zs[:], in_=values[:].rearrange("p o j t -> p (o j t)")
+            )
+            tiles_per_bank = N // P // len(banks)
+            o_sb = [keep.tile([P, 2, width], F32, name=f"o_sb{name}_{pair}") for pair in range(2)]
+            for n, b in enumerate(banks):
+                o_ps = bank(b, [P, tiles_per_bank, width])
+                for a in range(tiles_per_bank):
+                    rows = slice((n * tiles_per_bank + a) * P, (n * tiles_per_bank + a + 1) * P)
                     for i in range(2):
                         nc.tensor.matmul_mx(
                             out=o_ps[:, a, :],
@@ -210,62 +223,53 @@ def tile_picked_ace8_none_p_kernel(
                             start=(i == 0),
                             stop=(i == 1),
                         )
-                o_sb = keep.tile([P, 2, width], F32, name=f"o_sb{name}_{half}")
-                copies[half](o_sb[:], o_ps[:])
-                nc.sync.dma_start(out_v[:, 2 * half : 2 * half + 2, first : first + width], o_sb[:])
+                pair, at = divmod(n * tiles_per_bank, 2)
+                copies[n](o_sb[pair][:, at : at + tiles_per_bank, :], o_ps[:])
+                if at + tiles_per_bank == 2:
+                    nc.sync.dma_start(out_v[:, 2 * pair : 2 * pair + 2, first : first + width], o_sb[pair][:])
 
-        a_blk = [bank(2 + b, [P, P, PACK]) for b in range(4)]
-        zi_a = keep.tile([P, 2, HALF, PACK], BF16, name="zi_a", align_bytes=64)
-        z2_rows = [keep.tile([P, PACK, P], BF16, name=f"z2_rows{b}") for b in range(2)]
+        sums = [bank(b, [P, P, PACK]) for b in SUM_BANKS]
+        values_a = keep.tile([P, 2, HALF, PACK], BF16, name="values_a", align_bytes=64)
+        z2_planes = keep.tile([P, PACK, P], BF16, name="z2_planes", tag="z2_planes", align_bytes=64)
 
-        def sign_rows(t):
-            nc.scalar.activation(w3_signed[:, t, :], w_raw[1][:, t, :], COPY, scale=sign[:, t : t + 1])
+        def z2_plane(t):
+            nc.scalar.activation(z2_planes[:, t, :], sums[0][:, :, t], COPY, scale=ratio[:, t : t + 1])
 
-        def z2_plane(b, t):
-            nc.scalar.activation(z2_rows[b][:, t, :], a_blk[b][:, :, t], COPY, scale=ratio[:, t : t + 1])
+        def square_block_1():
+            second_order(values_a[:, 1, P:HALF, :], 1)
 
-        def z2_weave(b):
-            nc.scalar.copy(
-                zi_a[:, 0, b * P : (b + 1) * P, :].rearrange("p (c i) t -> p c t i", i=4),
-                z2_rows[b][:].rearrange("p t (c i) -> p c t i", i=4),
+        def square_block_0():
+            second_order(values_a[:, 1, 0:P, :], 0)
+            first_order(values_a[:, 0, P:HALF, :], 1)
+
+        def weave_z2():
+            weave(values_a[:, 0, 0:P, :], z2_planes[:])
+            quantize_weights(0, "z2_planes")
+
+        weight_jobs = (
+            [lambda q=q: weave_weights(0, w2_raw, q) for q in range(PACK)]
+            + [lambda t=t: sign_rows(t) for t in range(PACK)]
+            + [lambda q=q: weave_weights(1, w3_signed, q) for q in range(PACK)]
+        )
+        early = 1 + JOBS_PER_UNIT * PACK
+        jobs = weight_jobs[:early] + [square_block_1, square_block_0, weave_z2] + weight_jobs[early:]
+
+        jobs[0]()
+        for u in range(len(units)):
+            sum_unit(u)
+            if 1 <= u <= PACK:
+                z2_plane(u - 1)
+            for job in jobs[1 + JOBS_PER_UNIT * u : 1 + JOBS_PER_UNIT * (u + 1)]:
+                job()
+
+        quantize_weights(1, f"y{PACK - 1}")
+        last_product("a", values_a, last_term_tag, 0, (0, 6, 1, 7), (nc.scalar.copy,) * 4)
+        values_b = [keep.tile([P, 2, P, PACK], BF16, name=f"values_b{b}", align_bytes=64) for b in range(2)]
+        for b in range(2):
+            second_order(values_b[b][:, 1], 2 + b)
+        for b in range(2):
+            first_order(values_b[b][:, 0], 2 + b)
+        for b, banks in enumerate((SUM_BANKS[:2], SUM_BANKS[2:])):
+            last_product(
+                f"b{b}", values_b[b], f"zqb{b}", HALF + b * P, banks, (nc.scalar.copy, nc.vector.tensor_copy)
             )
-
-        weave_weights(0, w_raw[0], 0, nc.scalar.copy)
-        sum_plane(0, 0, 2)
-        weave_weights(0, w_raw[0], 1, nc.scalar.copy)
-        weave_weights(0, w_raw[0], 2, nc.scalar.copy)
-        sum_plane(1, 0, 2)
-        z2_plane(0, 0)
-        weave_weights(0, w_raw[0], 3, nc.scalar.copy)
-        quantize_weights(0, "w_q0")
-        sign_rows(0)
-        sum_plane(2, 0, 2)
-        z2_plane(0, 1)
-        sign_rows(1)
-        sign_rows(2)
-        sum_plane(3, 0, 2)
-        z2_plane(0, 2)
-        sign_rows(3)
-        weave_weights(1, w3_signed, 0, nc.scalar.copy)
-        sum_plane(0, 2, 2)
-        z2_plane(0, 3)
-        second_order(zi_a[:, 1, 1 * P : 2 * P, :], a_blk[1])
-        second_order(zi_a[:, 1, 0 * P : 1 * P, :], a_blk[0])
-        first_order(zi_a[:, 0, 1 * P : 2 * P, :], a_blk[1])
-        sum_plane(1, 2, 2)
-        z2_weave(0)
-        weave_weights(1, w3_signed, 1, nc.scalar.copy)
-        sum_plane(2, 2, 2)
-        weave_weights(1, w3_signed, 2, nc.scalar.copy)
-        weave_weights(1, w3_signed, 3, nc.scalar.copy)
-        sum_plane(3, 2, 1)
-        sum_plane(3, 3, 1)
-        quantize_weights(1, "y3")
-        last_product("a", zi_a, 0, HALF, (0, 6), (nc.scalar.copy, nc.scalar.copy))
-        zi_b = [keep.tile([P, 2, P, PACK], BF16, name=f"zi_b{b}", align_bytes=64) for b in range(2)]
-        for b in range(2):
-            second_order(zi_b[b][:, 1], a_blk[2 + b])
-        for b in range(2):
-            first_order(zi_b[b][:, 0], a_blk[2 + b])
-        last_product("b0", zi_b[0], HALF, P, (1, 7), (nc.scalar.copy, nc.vector.tensor_copy))
-        last_product("b1", zi_b[1], HALF + P, P, (2, 3), (nc.scalar.copy, nc.vector.tensor_copy))

@@ -25,10 +25,9 @@ PACK = 4
 HALF = S // 2
 LIST_ROWS = 16
 TERMS = 3
-TINY = 2.0**-120
+TINY = 2.0**-110
 GPSIMD_CLEARS = 640
-JOBS_PER_UNIT = 2
-ADD_BANKS = ((0, 1), (6, 7))
+WHOLE_PLANES = 2
 SUM_BANKS = (2, 3, 4, 5)
 
 
@@ -54,7 +53,7 @@ def tile_picked_ace8_none_p_kernel(
             return gt
 
         def load_rows(name, src):
-            wr = keep.tile([P, PACK, src.shape[1]], F32, name=name, tag=name)
+            wr = keep.tile([P, PACK, src.shape[1]], F32, name=name, tag=name, align_bytes=64)
             nc.sync.dma_start(wr[:], src.rearrange("(p j) c -> p j c", j=PACK))
             return wr
 
@@ -63,31 +62,32 @@ def tile_picked_ace8_none_p_kernel(
             nc.sync.dma_start(ct[:], src.rearrange("(p t) o -> p (t o)", t=PACK))
             return ct
 
-        xs = keep.tile([P, T], U8, name="xs", align_bytes=64)
+        xs = keep.tile([P, T], U8, name="xs", tag="xs", align_bytes=64)
         nc.gpsimd.memset(xs[:, 0:GPSIMD_CLEARS].bitcast(I32), 0)
         nc.vector.memset(xs[:, GPSIMD_CLEARS:T].bitcast(I32), 0)
         offs_t = load_list("offs_t", offs)
         c2_t = load_factor("c2_t", c2)
-        xw = keep.tile([P, T], I32, name="xw", align_bytes=64)
-        nc.sync.dma_start(xw[:], x_words[0].rearrange("p n t -> p (n t)").bitcast(I32))
+        w1_raw = load_rows("w1_raw", w1)
         for q in range(4):
             nc.sync.dma_start(
                 xs[32 * q : 32 * q + 4, :].bitcast(I32), x_scales[0, 4 * q : 4 * q + 4, :].bitcast(I32)
             )
-        w1_raw = load_rows("w1_raw", w1)
+        xw = keep.tile([P, T], I32, name="xw", tag="xw", align_bytes=64)
+        nc.sync.dma_start(xw[:], x_words[0].rearrange("p n t -> p (n t)").bitcast(I32))
+        c1_t = load_factor("c1_t", c1)
         lists, gains = [], []
         for k, (list_k, gain_k) in enumerate(((p1, g1), (p2, g2), (p3, g3))):
             lists.append(load_list(f"list{k}", list_k))
             gains.append(load_gain(f"gain{k}", gain_k))
-        w2_raw = load_rows("w2_raw", w2)
-        c1_t = load_factor("c1_t", c1)
+            if k == 0:
+                w2_raw = load_rows("w2_raw", w2)
         w3_raw = load_rows("w3_raw", w3)
 
         ident = keep.tile([P, P], F32, name="ident")
         make_identity(nc, ident[:])
 
         mag, root, sign, inv_root, ratio = (
-            keep.tile([P, PACK], F32, name=name) for name in ("mag", "root", "sign", "inv_root", "ratio")
+            keep.tile([P, PACK], F32, name=name, tag=name, align_bytes=64) for name in ("mag", "root", "sign", "inv_root", "ratio")
         )
         nc.scalar.activation(mag[:], c2_t[:], ABS)
         nc.scalar.activation(root[:], mag[:], SQRT, bias=TINY)
@@ -95,58 +95,72 @@ def tile_picked_ace8_none_p_kernel(
         nc.vector.reciprocal(inv_root[:], root[:])
 
         w1_b = keep.tile([P, PACK, P, PACK], BF16, name="w1_b", align_bytes=64)
-        w1_q = keep.tile([P, H], U32, name="w1_q", align_bytes=64)
+        w1_q = []
         w1_s = keep.tile([P, H], U8, name="w1_s", align_bytes=64)
         w1_from = w1_raw[:].rearrange("p j (m t) -> p m t j", t=PACK)
         w1_to = w1_b[:].rearrange("p t m j -> p m t j")
-        xw_g = keep.tile([P, S], U32, name="xw_g", align_bytes=64)
-        nc.vector.tensor_copy(xw_g[:], xw[:].bitcast(U32).indirect(offs_t[:]))
-        xs_g = keep.tile([P, S], U8, name="xs_g", align_bytes=64)
-        nc.vector.tensor_copy(xs_g[:], xs[:].indirect(offs_t[:]))
 
-        def quantize_w1(first, count):
+        def quantize_w1(first, count, tag):
             cols = slice(first * P, (first + count) * P)
+            w1_q.append(keep.tile([P, count * P], U32, name=f"w1_q{first}", tag=tag, align_bytes=64))
             nc.vector.quantize_mx(
-                out=w1_q[:, cols].bitcast(FP8X4),
+                out=w1_q[-1][:].bitcast(FP8X4),
                 scales=w1_s[:, cols],
                 in_=w1_b[:, first : first + count].rearrange("p t m j -> p (t m j)"),
             )
 
-        nc.vector.tensor_copy(w1_to[:, :, 0:2, :], w1_from[:, :, 0:2, :])
+        nc.scalar.copy(w1_to[:, :, 0:2, :], w1_from[:, :, 0:2, :])
         nc.scalar.copy(w1_to[:, :, 2:4, :], w1_from[:, :, 2:4, :])
-        quantize_w1(0, 1)
-        quantize_w1(1, 1)
-        quantize_w1(2, 2)
+        xs_g = keep.tile([P, S], U8, name="xs_g", align_bytes=64)
+        nc.vector.tensor_copy(xs_g[:], xs[:].indirect(offs_t[:]))
+        quantize_w1(0, 2, "xs")
+        xw_g = [keep.tile([P, HALF], U32, name=f"xw_g{h}", align_bytes=64) for h in range(2)]
+        for h in range(2):
+            nc.vector.tensor_copy(
+                xw_g[h][:],
+                xw[:].bitcast(U32).indirect(offs_t[:, h * HALF // LIST_ROWS : (h + 1) * HALF // LIST_ROWS]),
+            )
+        quantize_w1(2, 2, "xw")
 
-        def first_product(ps, t, cols):
+        def first_product(ps, t, lo, width):
+            cols = slice(lo, lo + width)
             nc.tensor.matmul_mx(
                 out=ps,
-                lhsT=w1_q[:, t * P : (t + 1) * P].bitcast(FP8X4),
+                lhsT=w1_q[t // 2][:, t % 2 * P : (t % 2 + 1) * P].bitcast(FP8X4),
                 lhsT_scale=w1_s[:, t * P : (t + 1) * P],
-                rhs=xw_g[:, cols].bitcast(FP8X4),
+                rhs=xw_g[lo // HALF][:, lo % HALF : lo % HALF + width].bitcast(FP8X4),
                 rhs_scale=xs_g[:, cols],
                 start=True,
                 stop=True,
             )
 
-        y = [keep.tile([P, S], F32, name=f"y{t}", tag=f"y{t}", align_bytes=64) for t in range(PACK)]
-        ps = bank(0, [P, HALF])
-        first_product(ps[:], 0, slice(0, HALF))
-        nc.scalar.activation(y[0][:, 0:HALF], ps[:], COPY, scale=root[:, 0:1])
-        ps = bank(1, [P, HALF])
-        first_product(ps[:], 0, slice(HALF, S))
-        nc.vector.tensor_scalar(y[0][:, HALF:S], ps[:], root[:, 0:1], None, MULT)
-        for t, b in zip(range(1, PACK), ADD_BANKS[1] + SUM_BANKS[:1]):
-            ps = bank(b, [P, S])
-            first_product(ps[:], t, slice(0, S))
-            nc.scalar.activation(y[t][:], ps[:], COPY, scale=root[:, t : t + 1])
+        y = []
+        for t in range(PACK):
+            wide = t < WHOLE_PLANES
+            y.append(keep.tile([P, 2 * S if wide else S], F32, name=f"y{t}", tag=f"y{t}", align_bytes=64))
+            if wide:
+                nc.gpsimd.memset(y[t][:, S : 2 * S], 0.0)
         for t in range(PACK):
             nc.scalar.activation(ratio[:, t : t + 1], c1_t[:, t : t + 1], COPY, scale=inv_root[:, t : t + 1])
+        ps = bank(0, [P, HALF])
+        first_product(ps[:], 0, 0, HALF)
+        nc.scalar.activation(y[0][:, 0:HALF], ps[:], COPY, scale=root[:, 0:1])
+        ps = bank(1, [P, P])
+        first_product(ps[:], 0, HALF, P)
+        nc.vector.tensor_scalar(y[0][:, HALF : HALF + P], ps[:], root[:, 0:1], None, MULT)
+        ps = bank(3, [P, P])
+        first_product(ps[:], 0, HALF + P, P)
+        nc.scalar.activation(y[0][:, HALF + P : S], ps[:], COPY, scale=root[:, 0:1])
+        for t, b in zip(range(1, PACK), (6, 7, 2)):
+            ps = bank(b, [P, S])
+            for lo in (HALF, 0):
+                first_product(ps[:, lo : lo + HALF], t, lo, HALF)
+            nc.scalar.activation(y[t][:, 0:S], ps[:], COPY, scale=root[:, t : t + 1])
 
-        w_b = [keep.tile([P, N, PACK], BF16, name=f"w_b{i}", align_bytes=64) for i in range(2)]
+        w_b = [keep.tile([P, N, PACK], BF16, name=f"w_b{i}", tag=f"w_b{i}", align_bytes=64) for i in range(2)]
         w_q = []
         w_s = [keep.tile([P, N], U8, name=f"w_s{i}", align_bytes=64) for i in range(2)]
-        w3_signed = keep.tile([P, PACK, N], BF16, name="w3_signed")
+        w3_signed = keep.tile([P, PACK, N], BF16, name="w3_signed", tag="w3_signed")
 
         def weave(dst, rows):
             nc.scalar.copy(
@@ -166,31 +180,37 @@ def tile_picked_ace8_none_p_kernel(
                 out=w_q[i][:].bitcast(FP8X4), scales=w_s[i][:], in_=w_b[i][:].rearrange("p m t -> p (m t)")
             )
 
-        units = [(t, first, 2) for first in (0, 2) for t in range(PACK)]
-        units = units[:-1] + [(PACK - 1, 2, 1), (PACK - 1, 3, 1)]
-        last_term_tag = f"term{TERMS * len(units) - 1}"
         out_v = out.rearrange("(a p) j -> p a j", p=P)
 
-        def sum_unit(u):
-            t, first, blocks = units[u]
+        half_terms = []
+
+        def term_buffer(t, first, n):
+            if t < WHOLE_PLANES:
+                slot = (0, 1, 2, 3, 2, 3)[TERMS * t + n]
+                return keep.tile([P, S], F32, name="term", tag=f"term{slot}", align_bytes=64)[:]
+            if not half_terms:
+                half_terms.append(keep.tile([P, 2, 2, TERMS, HALF], F32, name="half_terms", tag="term2", align_bytes=64))
+            return half_terms[0][:, t - WHOLE_PLANES, first // 2, n, :]
+
+        def sum_unit(t, first, blocks, add_bank, turned_tag):
             lo, width = first * P, blocks * P
-            turned_ps = [bank(ADD_BANKS[u % 2][b], [P, P]) for b in range(blocks)]
-            for k in range(TERMS):
-                term = keep.tile([P, width], F32, name="term", tag=f"term{TERMS * u + k}", align_bytes=64)
+            turned_ps = bank(add_bank, [P, blocks, P])
+            order = (2, 0, 1) if t == 1 else range(TERMS)
+            for n, k in enumerate(order):
+                term = term_buffer(t, first, n)
                 nc.vector.tensor_tensor(
-                    term[:],
+                    term,
                     y[t][:].indirect(lists[k][:, lo // LIST_ROWS : (lo + width) // LIST_ROWS]),
                     gains[k][:, lo : lo + width],
                     MULT,
                 )
                 for b in range(blocks):
                     nc.tensor.matmul(
-                        turned_ps[b][:], term[:, b * P : (b + 1) * P], ident[:],
-                        start=(k == 0), stop=(k == TERMS - 1), is_transpose=True,
+                        turned_ps[:, b, :], term[:, b * P : (b + 1) * P], ident[:],
+                        start=(n == 0 and b == 0), stop=(n == TERMS - 1 and b == blocks - 1), is_transpose=True,
                     )
-            turned = keep.tile([P, blocks, P], F32, name="turned", tag=f"turned{u % 2}")
-            for b in range(blocks):
-                nc.scalar.copy(turned[:, b, :], turned_ps[b][:])
+            turned = keep.tile([P, blocks, P], F32, name="turned", tag=turned_tag, align_bytes=64)
+            nc.scalar.copy(turned[:], turned_ps[:])
             for b in range(blocks):
                 nc.tensor.transpose(sums[first + b][:, :, t], turned[:, b, :], ident[:])
 
@@ -200,13 +220,16 @@ def tile_picked_ace8_none_p_kernel(
         def second_order(dst, b):
             nc.scalar.activation(dst, sums[b][:], SQUARE)
 
-        def last_product(name, values, codes_tag, first, banks, copies):
+        def quantize_values(name, values, tag):
             width = values.shape[2]
-            zq = keep.tile([P, 2 * width], U32, name=f"zq{name}", tag=codes_tag, align_bytes=64)
+            zq = keep.tile([P, 2 * width], U32, name=f"zq{name}", tag=tag, align_bytes=64)
             zs = keep.tile([P, 2 * width], U8, name=f"zs{name}", align_bytes=64)
             nc.vector.quantize_mx(
                 out=zq[:].bitcast(FP8X4), scales=zs[:], in_=values[:].rearrange("p o j t -> p (o j t)")
             )
+            return zq, zs
+
+        def last_product(name, zq, zs, width, first, banks, copies):
             tiles_per_bank = N // P // len(banks)
             o_sb = [keep.tile([P, 2, width], F32, name=f"o_sb{name}_{pair}") for pair in range(2)]
             for n, b in enumerate(banks):
@@ -229,47 +252,44 @@ def tile_picked_ace8_none_p_kernel(
                     nc.sync.dma_start(out_v[:, 2 * pair : 2 * pair + 2, first : first + width], o_sb[pair][:])
 
         sums = [bank(b, [P, P, PACK]) for b in SUM_BANKS]
-        values_a = keep.tile([P, 2, HALF, PACK], BF16, name="values_a", align_bytes=64)
+        values_a = keep.tile([P, 2, HALF, PACK], BF16, name="values_a", tag="values_a", align_bytes=64)
+        values_b = [keep.tile([P, 2, P, PACK], BF16, name=f"values_b{b}", align_bytes=64) for b in range(2)]
+
         z2_planes = keep.tile([P, PACK, P], BF16, name="z2_planes", tag="z2_planes", align_bytes=64)
 
         def z2_plane(t):
             nc.scalar.activation(z2_planes[:, t, :], sums[0][:, :, t], COPY, scale=ratio[:, t : t + 1])
 
-        def square_block_1():
-            second_order(values_a[:, 1, P:HALF, :], 1)
-
-        def square_block_0():
-            second_order(values_a[:, 1, 0:P, :], 0)
-            first_order(values_a[:, 0, P:HALF, :], 1)
-
-        def weave_z2():
-            weave(values_a[:, 0, 0:P, :], z2_planes[:])
-            quantize_weights(0, "z2_planes")
-
-        weight_jobs = (
-            [lambda q=q: weave_weights(0, w2_raw, q) for q in range(PACK)]
-            + [lambda t=t: sign_rows(t) for t in range(PACK)]
-            + [lambda q=q: weave_weights(1, w3_signed, q) for q in range(PACK)]
-        )
-        early = 1 + JOBS_PER_UNIT * PACK
-        jobs = weight_jobs[:early] + [square_block_1, square_block_0, weave_z2] + weight_jobs[early:]
-
-        jobs[0]()
-        for u in range(len(units)):
-            sum_unit(u)
-            if 1 <= u <= PACK:
-                z2_plane(u - 1)
-            for job in jobs[1 + JOBS_PER_UNIT * u : 1 + JOBS_PER_UNIT * (u + 1)]:
-                job()
-
-        quantize_weights(1, f"y{PACK - 1}")
-        last_product("a", values_a, last_term_tag, 0, (0, 6, 1, 7), (nc.scalar.copy,) * 4)
-        values_b = [keep.tile([P, 2, P, PACK], BF16, name=f"values_b{b}", align_bytes=64) for b in range(2)]
+        for q in range(PACK):
+            weave_weights(0, w2_raw, q)
+        for t in range(PACK):
+            sign_rows(t)
+        sum_unit(0, 0, 4, 0, "w2_raw")
+        for q in range(2):
+            weave_weights(1, w3_signed, q)
+        sum_unit(1, 0, 4, 1, "w3_raw")
+        for q in range(2, PACK):
+            weave_weights(1, w3_signed, q)
+        sum_unit(2, 0, 2, 0, "sign")
+        z2_plane(0)
+        z2_plane(1)
+        sum_unit(3, 0, 2, 1, "turned_a3")
+        z2_plane(2)
+        for b in (1, 0):
+            second_order(values_a[:, 1, b * P : (b + 1) * P, :], b)
+        sum_unit(2, 2, 2, 1, "turned_b2")
+        z2_plane(3)
+        weave(values_a[:, 0, 0:P, :], z2_planes[:])
+        sum_unit(3, 2, 2, 1, "turned_b3")
+        first_order(values_a[:, 0, P:HALF, :], 1)
+        quantize_weights(0, "z2_planes")
+        zq_a, zs_a = quantize_values("a", values_a, "term2")
+        quantize_weights(1, "values_a")
         for b in range(2):
             second_order(values_b[b][:, 1], 2 + b)
+        last_product("a", zq_a, zs_a, HALF, 0, (6, 7, 0, 1), (nc.scalar.copy,) * 4)
         for b in range(2):
             first_order(values_b[b][:, 0], 2 + b)
         for b, banks in enumerate((SUM_BANKS[:2], SUM_BANKS[2:])):
-            last_product(
-                f"b{b}", values_b[b], f"zqb{b}", HALF + b * P, banks, (nc.scalar.copy, nc.vector.tensor_copy)
-            )
+            zq, zs = quantize_values(f"b{b}", values_b[b], f"zqb{b}")
+            last_product(f"b{b}", zq, zs, P, HALF + b * P, banks, (nc.scalar.copy, nc.vector.tensor_copy))

@@ -79,8 +79,7 @@ def tile_picked_ace8_none_p_kernel(
         for k, (list_k, gain_k) in enumerate(((p1, g1), (p2, g2), (p3, g3))):
             lists.append(load_list(f"list{k}", list_k))
             gains.append(load_gain(f"gain{k}", gain_k))
-            if k == 0:
-                w2_raw = load_rows("w2_raw", w2)
+        w2_raw = load_rows("w2_raw", w2)
         w3_raw = load_rows("w3_raw", w3)
 
         ident = keep.tile([P, P], F32, name="ident")

@@ -144,12 +144,10 @@ def tile_picked_ace8_none_p_kernel(
         ps = bank(0, [P, HALF])
         first_product(ps[:], 0, 0, HALF)
         nc.scalar.activation(y[0][:, 0:HALF], ps[:], COPY, scale=root[:, 0:1])
-        ps = bank(1, [P, P])
-        first_product(ps[:], 0, HALF, P)
-        nc.vector.tensor_scalar(y[0][:, HALF : HALF + P], ps[:], root[:, 0:1], None, MULT)
-        ps = bank(3, [P, P])
-        first_product(ps[:], 0, HALF + P, P)
-        nc.scalar.activation(y[0][:, HALF + P : S], ps[:], COPY, scale=root[:, 0:1])
+        for b, lo in ((1, HALF), (3, HALF + P)):
+            ps = bank(b, [P, P])
+            first_product(ps[:], 0, lo, P)
+            nc.scalar.activation(y[0][:, lo : lo + P], ps[:], COPY, scale=root[:, 0:1])
         for t, b in zip(range(1, PACK), (6, 7, 2)):
             ps = bank(b, [P, S])
             for lo in (HALF, 0):
@@ -157,7 +155,6 @@ def tile_picked_ace8_none_p_kernel(
             nc.scalar.activation(y[t][:, 0:S], ps[:], COPY, scale=root[:, t : t + 1])
 
         w_b = [keep.tile([P, N, PACK], BF16, name=f"w_b{i}", tag=f"w_b{i}", align_bytes=64) for i in range(2)]
-        w_q = []
         w_s = [keep.tile([P, N], U8, name=f"w_s{i}", align_bytes=64) for i in range(2)]
         w3_signed = keep.tile([P, PACK, N], BF16, name="w3_signed", tag="w3_signed")
 
@@ -173,10 +170,9 @@ def tile_picked_ace8_none_p_kernel(
         def sign_rows(t):
             nc.scalar.activation(w3_signed[:, t, :], w3_raw[:, t, :], COPY, scale=sign[:, t : t + 1])
 
-        def quantize_weights(i, tag):
-            w_q.append(keep.tile([P, N], U32, name=f"w_q{i}", tag=tag, align_bytes=64))
+        def quantize_weights(i):
             nc.vector.quantize_mx(
-                out=w_q[i][:].bitcast(FP8X4), scales=w_s[i][:], in_=w_b[i][:].rearrange("p m t -> p (m t)")
+                out=w_q[:, i, :].bitcast(FP8X4), scales=w_s[i][:], in_=w_b[i][:].rearrange("p m t -> p (m t)")
             )
 
         out_v = out.rearrange("(a p) j -> p a j", p=P)
@@ -228,27 +224,26 @@ def tile_picked_ace8_none_p_kernel(
             )
             return zq, zs
 
-        def last_product(name, zq, zs, width, first, banks, copies):
-            tiles_per_bank = N // P // len(banks)
-            o_sb = [keep.tile([P, 2, width], F32, name=f"o_sb{name}_{pair}") for pair in range(2)]
+        def last_product(name, zq, zs, width, first, pair, banks, copies):
+            tiles_per_bank = 2 // len(banks)
+            o_sb = keep.tile([P, 2, width], F32, name=f"o_sb{name}_{pair}")
             for n, b in enumerate(banks):
                 o_ps = bank(b, [P, tiles_per_bank, width])
                 for a in range(tiles_per_bank):
-                    rows = slice((n * tiles_per_bank + a) * P, (n * tiles_per_bank + a + 1) * P)
+                    tile_number = 2 * pair + n * tiles_per_bank + a
+                    rows = slice(tile_number * P, (tile_number + 1) * P)
                     for i in range(2):
                         nc.tensor.matmul_mx(
                             out=o_ps[:, a, :],
-                            lhsT=w_q[i][:, rows].bitcast(FP8X4),
+                            lhsT=w_q[:, i, rows].bitcast(FP8X4),
                             lhsT_scale=w_s[i][:, rows],
                             rhs=zq[:, i * width : (i + 1) * width].bitcast(FP8X4),
                             rhs_scale=zs[:, i * width : (i + 1) * width],
                             start=(i == 0),
                             stop=(i == 1),
                         )
-                pair, at = divmod(n * tiles_per_bank, 2)
-                copies[n](o_sb[pair][:, at : at + tiles_per_bank, :], o_ps[:])
-                if at + tiles_per_bank == 2:
-                    nc.sync.dma_start(out_v[:, 2 * pair : 2 * pair + 2, first : first + width], o_sb[pair][:])
+                copies[n](o_sb[:, n * tiles_per_bank : (n + 1) * tiles_per_bank, :], o_ps[:])
+            nc.sync.dma_start(out_v[:, 2 * pair : 2 * pair + 2, first : first + width], o_sb[:])
 
         sums = [bank(b, [P, P, PACK]) for b in SUM_BANKS]
         values_a = keep.tile([P, 2, HALF, PACK], BF16, name="values_a", tag="values_a", align_bytes=64)
@@ -281,14 +276,17 @@ def tile_picked_ace8_none_p_kernel(
         weave(values_a[:, 0, 0:P, :], z2_planes[:])
         sum_unit(3, 2, 2, 1, "turned_b3")
         first_order(values_a[:, 0, P:HALF, :], 1)
-        quantize_weights(0, "z2_planes")
+        w_q = keep.tile([P, 2, N], U32, name="w_q", tag="z2_planes", align_bytes=64)
+        quantize_weights(0)
         zq_a, zs_a = quantize_values("a", values_a, "term2")
-        quantize_weights(1, "values_a")
+        quantize_weights(1)
         for b in range(2):
             second_order(values_b[b][:, 1], 2 + b)
-        last_product("a", zq_a, zs_a, HALF, 0, (6, 7, 0, 1), (nc.scalar.copy,) * 4)
         for b in range(2):
             first_order(values_b[b][:, 0], 2 + b)
+        last_product("a", zq_a, zs_a, HALF, 0, 0, (6, 7), (nc.scalar.copy,) * 2)
+        last_product("a", zq_a, zs_a, HALF, 0, 1, (0, 1), (nc.scalar.copy,) * 2)
         for b, banks in enumerate((SUM_BANKS[:2], SUM_BANKS[2:])):
             zq, zs = quantize_values(f"b{b}", values_b[b], f"zqb{b}")
-            last_product(f"b{b}", zq, zs, P, HALF + b * P, banks, (nc.scalar.copy, nc.vector.tensor_copy))
+            for pair, copy in enumerate((nc.scalar.copy, nc.vector.tensor_copy)):
+                last_product(f"b{b}", zq, zs, P, HALF + b * P, pair, banks[pair : pair + 1], (copy,))

@@ -269,16 +269,18 @@ def tile_picked_ace8_none_p_kernel(
         z2_plane(1)
         sum_unit(3, 0, 2, 1, "turned_a3")
         z2_plane(2)
+        sum_unit(2, 2, 2, 0, "turned_b2")
+        z2_plane(3)
         for b in (1, 0):
             second_order(values_a[:, 1, b * P : (b + 1) * P, :], b)
-        sum_unit(2, 2, 2, 1, "turned_b2")
-        z2_plane(3)
-        weave(values_a[:, 0, 0:P, :], z2_planes[:])
         sum_unit(3, 2, 2, 1, "turned_b3")
         first_order(values_a[:, 0, P:HALF, :], 1)
-        w_q = keep.tile([P, 2, N], U32, name="w_q", tag="z2_planes", align_bytes=64)
+        nc.vector.tensor_copy(
+            values_a[:, 0, 0:P, :].rearrange("p (c i) t -> p c t i", i=4), z2_planes[:].rearrange("p t (c i) -> p c t i", i=4)
+        )
+        w_q = keep.tile([P, 2, N], U32, name="w_q", tag="term2", align_bytes=64)
         quantize_weights(0)
-        zq_a, zs_a = quantize_values("a", values_a, "term2")
+        zq_a, zs_a = quantize_values("a", values_a, "zq_a")
         quantize_weights(1)
         for b in range(2):
             second_order(values_b[b][:, 1], 2 + b)

@@ -25,6 +25,7 @@ PACK = 4
 HALF = S // 2
 LIST_ROWS = 16
 TERMS = 3
+LAST_PLANE = PACK - 1
 TINY = 2.0**-110
 GPSIMD_CLEARS = 640
 WHOLE_PLANES = 2
@@ -86,7 +87,8 @@ def tile_picked_ace8_none_p_kernel(
         make_identity(nc, ident[:])
 
         mag, root, sign, inv_root, ratio = (
-            keep.tile([P, PACK], F32, name=name, tag=name, align_bytes=64) for name in ("mag", "root", "sign", "inv_root", "ratio")
+            keep.tile([P, PACK], F32, name=name, tag=name, align_bytes=64)
+            for name in ("mag", "root", "sign", "inv_root", "ratio")
         )
         nc.scalar.activation(mag[:], c2_t[:], ABS)
         nc.scalar.activation(root[:], mag[:], SQRT, bias=TINY)
@@ -99,36 +101,34 @@ def tile_picked_ace8_none_p_kernel(
         w1_from = w1_raw[:].rearrange("p j (m t) -> p m t j", t=PACK)
         w1_to = w1_b[:].rearrange("p t m j -> p m t j")
 
-        def quantize_w1(first, count, tag):
-            cols = slice(first * P, (first + count) * P)
-            w1_q.append(keep.tile([P, count * P], U32, name=f"w1_q{first}", tag=tag, align_bytes=64))
+        def quantize_w1(pair, tag):
+            w1_q.append(keep.tile([P, 2 * P], U32, name=f"w1_q{pair}", tag=tag, align_bytes=64))
             nc.vector.quantize_mx(
-                out=w1_q[-1][:].bitcast(FP8X4),
-                scales=w1_s[:, cols],
-                in_=w1_b[:, first : first + count].rearrange("p t m j -> p (t m j)"),
+                out=w1_q[pair][:].bitcast(FP8X4),
+                scales=w1_s[:, 2 * pair * P : 2 * (pair + 1) * P],
+                in_=w1_b[:, 2 * pair : 2 * pair + 2].rearrange("p t m j -> p (t m j)"),
             )
 
-        nc.scalar.copy(w1_to[:, :, 0:2, :], w1_from[:, :, 0:2, :])
-        nc.scalar.copy(w1_to[:, :, 2:4, :], w1_from[:, :, 2:4, :])
+        for pair in range(2):
+            nc.scalar.copy(w1_to[:, :, 2 * pair : 2 * pair + 2, :], w1_from[:, :, 2 * pair : 2 * pair + 2, :])
         xs_g = keep.tile([P, S], U8, name="xs_g", align_bytes=64)
         nc.vector.tensor_copy(xs_g[:], xs[:].indirect(offs_t[:]))
-        quantize_w1(0, 2, "xs")
+        quantize_w1(0, "xs")
         xw_g = [keep.tile([P, HALF], U32, name=f"xw_g{h}", align_bytes=64) for h in range(2)]
         for h in range(2):
             nc.vector.tensor_copy(
                 xw_g[h][:],
                 xw[:].bitcast(U32).indirect(offs_t[:, h * HALF // LIST_ROWS : (h + 1) * HALF // LIST_ROWS]),
             )
-        quantize_w1(2, 2, "xw")
+        quantize_w1(1, "xw")
 
         def first_product(ps, t, lo, width):
-            cols = slice(lo, lo + width)
             nc.tensor.matmul_mx(
                 out=ps,
                 lhsT=w1_q[t // 2][:, t % 2 * P : (t % 2 + 1) * P].bitcast(FP8X4),
                 lhsT_scale=w1_s[:, t * P : (t + 1) * P],
                 rhs=xw_g[lo // HALF][:, lo % HALF : lo % HALF + width].bitcast(FP8X4),
-                rhs_scale=xs_g[:, cols],
+                rhs_scale=xs_g[:, lo : lo + width],
                 start=True,
                 stop=True,
             )
@@ -136,27 +136,24 @@ def tile_picked_ace8_none_p_kernel(
         y = []
         for t in range(PACK):
             wide = t < WHOLE_PLANES
-            y.append(keep.tile([P, 2 * S if wide else S], F32, name=f"y{t}", tag=f"y{t}", align_bytes=64))
+            y.append(keep.tile([P, 2 * S if wide else S], F32, name=f"y{t}", align_bytes=64))
             if wide:
                 nc.gpsimd.memset(y[t][:, S : 2 * S], 0.0)
         for t in range(PACK):
             nc.scalar.activation(ratio[:, t : t + 1], c1_t[:, t : t + 1], COPY, scale=inv_root[:, t : t + 1])
-        ps = bank(0, [P, HALF])
-        first_product(ps[:], 0, 0, HALF)
-        nc.scalar.activation(y[0][:, 0:HALF], ps[:], COPY, scale=root[:, 0:1])
-        for b, lo in ((1, HALF), (3, HALF + P)):
-            ps = bank(b, [P, P])
-            first_product(ps[:], 0, lo, P)
-            nc.scalar.activation(y[0][:, lo : lo + P], ps[:], COPY, scale=root[:, 0:1])
+        for b, lo, width in ((0, 0, HALF), (1, HALF, P), (3, HALF + P, P)):
+            ps = bank(b, [P, width])
+            first_product(ps[:], 0, lo, width)
+            nc.scalar.activation(y[0][:, lo : lo + width], ps[:], COPY, scale=root[:, 0:1])
         for t, b in zip(range(1, PACK), (6, 7, 2)):
             ps = bank(b, [P, S])
             for lo in (HALF, 0):
                 first_product(ps[:, lo : lo + HALF], t, lo, HALF)
             nc.scalar.activation(y[t][:, 0:S], ps[:], COPY, scale=root[:, t : t + 1])
 
-        w_b = [keep.tile([P, N, PACK], BF16, name=f"w_b{i}", tag=f"w_b{i}", align_bytes=64) for i in range(2)]
+        w_b = [keep.tile([P, N, PACK], BF16, name=f"w_b{i}", align_bytes=64) for i in range(2)]
         w_s = [keep.tile([P, N], U8, name=f"w_s{i}", align_bytes=64) for i in range(2)]
-        w3_signed = keep.tile([P, PACK, N], BF16, name="w3_signed", tag="w3_signed")
+        w3_signed = keep.tile([P, PACK, N], BF16, name="w3_signed")
 
         def weave(dst, rows):
             nc.scalar.copy(
@@ -170,26 +167,25 @@ def tile_picked_ace8_none_p_kernel(
         def sign_rows(t):
             nc.scalar.activation(w3_signed[:, t, :], w3_raw[:, t, :], COPY, scale=sign[:, t : t + 1])
 
-        def quantize_weights(i):
-            nc.vector.quantize_mx(
-                out=w_q[:, i, :].bitcast(FP8X4), scales=w_s[i][:], in_=w_b[i][:].rearrange("p m t -> p (m t)")
-            )
-
-        out_v = out.rearrange("(a p) j -> p a j", p=P)
-
         half_terms = []
 
         def term_buffer(t, first, n):
             if t < WHOLE_PLANES:
-                slot = (0, 1, 2, 3, 2, 3)[TERMS * t + n]
+                number = TERMS * t + n
+                slot = number if number <= TERMS else 2 + number % 2
                 return keep.tile([P, S], F32, name="term", tag=f"term{slot}", align_bytes=64)[:]
+            if (t, first, n) == (LAST_PLANE, 2, TERMS - 1):
+                return keep.tile([P, HALF], F32, name="term", tag="term3", align_bytes=64)[:]
             if not half_terms:
-                half_terms.append(keep.tile([P, 2, 2, TERMS, HALF], F32, name="half_terms", tag="term2", align_bytes=64))
+                half_terms.append(
+                    keep.tile([P, 2, 2, TERMS, HALF], F32, name="half_terms", tag="term2", align_bytes=64)
+                )
             return half_terms[0][:, t - WHOLE_PLANES, first // 2, n, :]
 
-        def sum_unit(t, first, blocks, add_bank, turned_tag):
-            lo, width = first * P, blocks * P
-            turned_ps = bank(add_bank, [P, blocks, P])
+        def sum_unit(t, first, batches, add_bank, turned_tag):
+            lo, width = first * P, batches * P
+            per_copy = 1 if t == LAST_PLANE else batches
+            turned_ps = bank(add_bank, [P, batches, P])
             order = (2, 0, 1) if t == 1 else range(TERMS)
             for n, k in enumerate(order):
                 term = term_buffer(t, first, n)
@@ -199,15 +195,16 @@ def tile_picked_ace8_none_p_kernel(
                     gains[k][:, lo : lo + width],
                     MULT,
                 )
-                for b in range(blocks):
+                for b in range(batches):
                     nc.tensor.matmul(
                         turned_ps[:, b, :], term[:, b * P : (b + 1) * P], ident[:],
-                        start=(n == 0 and b == 0), stop=(n == TERMS - 1 and b == blocks - 1), is_transpose=True,
+                        start=(n == 0 and b == 0), stop=(n == TERMS - 1 and b == batches - 1), is_transpose=True,
                     )
-            turned = keep.tile([P, blocks, P], F32, name="turned", tag=turned_tag, align_bytes=64)
-            nc.scalar.copy(turned[:], turned_ps[:])
-            for b in range(blocks):
-                nc.tensor.transpose(sums[first + b][:, :, t], turned[:, b, :], ident[:])
+            turned = keep.tile([P, batches, P], F32, name="turned", tag=turned_tag, align_bytes=64)
+            for piece in range(0, batches, per_copy):
+                nc.scalar.copy(turned[:, piece : piece + per_copy, :], turned_ps[:, piece : piece + per_copy, :])
+                for b in range(piece, piece + per_copy):
+                    nc.tensor.transpose(sums[first + b][:, :, t], turned[:, b, :], ident[:])
 
         def first_order(dst, b):
             nc.vector.tensor_tensor(dst, sums[b][:], ratio[:].unsqueeze(1).to_broadcast([P, P, PACK]), MULT)
@@ -215,41 +212,10 @@ def tile_picked_ace8_none_p_kernel(
         def second_order(dst, b):
             nc.scalar.activation(dst, sums[b][:], SQUARE)
 
-        def quantize_values(name, values, tag):
-            width = values.shape[2]
-            zq = keep.tile([P, 2 * width], U32, name=f"zq{name}", tag=tag, align_bytes=64)
-            zs = keep.tile([P, 2 * width], U8, name=f"zs{name}", align_bytes=64)
-            nc.vector.quantize_mx(
-                out=zq[:].bitcast(FP8X4), scales=zs[:], in_=values[:].rearrange("p o j t -> p (o j t)")
-            )
-            return zq, zs
-
-        def last_product(name, zq, zs, width, first, pair, banks, copies):
-            tiles_per_bank = 2 // len(banks)
-            o_sb = keep.tile([P, 2, width], F32, name=f"o_sb{name}_{pair}")
-            for n, b in enumerate(banks):
-                o_ps = bank(b, [P, tiles_per_bank, width])
-                for a in range(tiles_per_bank):
-                    tile_number = 2 * pair + n * tiles_per_bank + a
-                    rows = slice(tile_number * P, (tile_number + 1) * P)
-                    for i in range(2):
-                        nc.tensor.matmul_mx(
-                            out=o_ps[:, a, :],
-                            lhsT=w_q[:, i, rows].bitcast(FP8X4),
-                            lhsT_scale=w_s[i][:, rows],
-                            rhs=zq[:, i * width : (i + 1) * width].bitcast(FP8X4),
-                            rhs_scale=zs[:, i * width : (i + 1) * width],
-                            start=(i == 0),
-                            stop=(i == 1),
-                        )
-                copies[n](o_sb[:, n * tiles_per_bank : (n + 1) * tiles_per_bank, :], o_ps[:])
-            nc.sync.dma_start(out_v[:, 2 * pair : 2 * pair + 2, first : first + width], o_sb[:])
-
         sums = [bank(b, [P, P, PACK]) for b in SUM_BANKS]
-        values_a = keep.tile([P, 2, HALF, PACK], BF16, name="values_a", tag="values_a", align_bytes=64)
+        values_a = keep.tile([P, 2, HALF, PACK], BF16, name="values_a", align_bytes=64)
         values_b = [keep.tile([P, 2, P, PACK], BF16, name=f"values_b{b}", align_bytes=64) for b in range(2)]
-
-        z2_planes = keep.tile([P, PACK, P], BF16, name="z2_planes", tag="z2_planes", align_bytes=64)
+        z2_planes = keep.tile([P, PACK, P], BF16, name="z2_planes", align_bytes=64)
 
         def z2_plane(t):
             nc.scalar.activation(z2_planes[:, t, :], sums[0][:, :, t], COPY, scale=ratio[:, t : t + 1])
@@ -269,26 +235,75 @@ def tile_picked_ace8_none_p_kernel(
         z2_plane(1)
         sum_unit(3, 0, 2, 1, "turned_a3")
         z2_plane(2)
-        sum_unit(2, 2, 2, 0, "turned_b2")
         z2_plane(3)
-        for b in (1, 0):
-            second_order(values_a[:, 1, b * P : (b + 1) * P, :], b)
-        sum_unit(3, 2, 2, 1, "turned_b3")
+        second_order(values_a[:, 1, 0:P, :], 0)
+        sum_unit(2, 2, 2, 1, "turned_b2")
+        second_order(values_a[:, 1, P:HALF, :], 1)
+        weave(values_a[:, 0, 0:P, :], z2_planes[:])
+        sum_unit(3, 2, 2, SUM_BANKS[0], "turned_b3")
         first_order(values_a[:, 0, P:HALF, :], 1)
-        nc.vector.tensor_copy(
-            values_a[:, 0, 0:P, :].rearrange("p (c i) t -> p c t i", i=4), z2_planes[:].rearrange("p t (c i) -> p c t i", i=4)
-        )
-        w_q = keep.tile([P, 2, N], U32, name="w_q", tag="term2", align_bytes=64)
+
+        codes = keep.tile([P, 3, N], U32, name="codes", tag="term2", align_bytes=64)
+        out_v = out.rearrange("(a p) j -> p a j", p=P)
+
+        def quantize_weights(i):
+            nc.vector.quantize_mx(
+                out=codes[:, i, :].bitcast(FP8X4), scales=w_s[i][:], in_=w_b[i][:].rearrange("p m t -> p (m t)")
+            )
+
+        def quantize_values(name, values, zq):
+            zs = keep.tile([P, 2 * values.shape[2]], U8, name=f"zs{name}", align_bytes=64)
+            nc.vector.quantize_mx(
+                out=zq.bitcast(FP8X4), scales=zs[:], in_=values[:].rearrange("p o j t -> p (o j t)")
+            )
+            return zs
+
+        def last_pass(o_ps, i, tile_number, zq, zs, start, stop):
+            width = o_ps.shape[1]
+            rows = slice(tile_number * P, (tile_number + 1) * P)
+            nc.tensor.matmul_mx(
+                out=o_ps,
+                lhsT=codes[:, i, rows].bitcast(FP8X4),
+                lhsT_scale=w_s[i][:, rows],
+                rhs=zq[:, i * width : (i + 1) * width].bitcast(FP8X4),
+                rhs_scale=zs[:, i * width : (i + 1) * width],
+                start=start,
+                stop=stop,
+            )
+
         quantize_weights(0)
-        zq_a, zs_a = quantize_values("a", values_a, "zq_a")
+        zq_a = codes[:, 2, :]
+        zs_a = quantize_values("a", values_a, zq_a)
         quantize_weights(1)
         for b in range(2):
             second_order(values_b[b][:, 1], 2 + b)
         for b in range(2):
             first_order(values_b[b][:, 0], 2 + b)
-        last_product("a", zq_a, zs_a, HALF, 0, 0, (6, 7), (nc.scalar.copy,) * 2)
-        last_product("a", zq_a, zs_a, HALF, 0, 1, (0, 1), (nc.scalar.copy,) * 2)
-        for b, banks in enumerate((SUM_BANKS[:2], SUM_BANKS[2:])):
-            zq, zs = quantize_values(f"b{b}", values_b[b], f"zqb{b}")
+
+        o_ps = bank(SUM_BANKS[0], [P, 2, HALF])
+        for i in range(2):
+            for a in range(2):
+                last_pass(o_ps[:, a, :], i, a, zq_a, zs_a, (i, a) == (0, 0), (i, a) == (1, 1))
+        o_sb = keep.tile([P, 2, HALF], F32, name="o_sba0")
+        nc.scalar.copy(o_sb[:], o_ps[:])
+        nc.sync.dma_start(out_v[:, 0:2, 0:HALF], o_sb[:])
+        o_sb = keep.tile([P, 2, HALF], F32, name="o_sba1")
+        for a, b in enumerate((6, 7)):
+            o_ps = bank(b, [P, HALF])
+            for i in (1, 0):
+                last_pass(o_ps[:], i, 2 + a, zq_a, zs_a, i == 1, i == 0)
+            nc.scalar.copy(o_sb[:, a, :], o_ps[:])
+        nc.sync.dma_start(out_v[:, 2:4, 0:HALF], o_sb[:])
+
+        for b, banks in enumerate(((0, 1), SUM_BANKS[2:])):
+            zq_b = keep.tile([P, 2 * P], U32, name=f"zq_b{b}", align_bytes=64)
+            zs_b = quantize_values(f"b{b}", values_b[b], zq_b[:])
             for pair, copy in enumerate((nc.scalar.copy, nc.vector.tensor_copy)):
-                last_product(f"b{b}", zq, zs, P, HALF + b * P, pair, banks[pair : pair + 1], (copy,))
+                o_ps = bank(banks[pair], [P, 2, P])
+                for a in range(2):
+                    for i in range(2):
+                        last_pass(o_ps[:, a, :], i, 2 * pair + a, zq_b[:], zs_b, i == 0, i == 1)
+                o_sb = keep.tile([P, 2, P], F32, name=f"o_sbb{b}_{pair}")
+                copy(o_sb[:], o_ps[:])
+                first = HALF + b * P
+                nc.sync.dma_start(out_v[:, 2 * pair : 2 * pair + 2, first : first + P], o_sb[:])

@@ -284,9 +284,10 @@ def tile_picked_ace8_none_p_kernel(
         for i in range(2):
             for a in range(2):
                 last_pass(o_ps[:, a, :], i, a, zq_a, zs_a, (i, a) == (0, 0), (i, a) == (1, 1))
-        o_sb = keep.tile([P, 2, HALF], F32, name="o_sba0")
-        nc.scalar.copy(o_sb[:], o_ps[:])
-        nc.sync.dma_start(out_v[:, 0:2, 0:HALF], o_sb[:])
+        for a in range(2):
+            o_sb = keep.tile([P, HALF], F32, name=f"o_sba0_{a}")
+            nc.scalar.copy(o_sb[:], o_ps[:, a, :])
+            nc.sync.dma_start(out_v[:, a, 0:HALF], o_sb[:])
         o_sb = keep.tile([P, 2, HALF], F32, name="o_sba1")
         for a, b in enumerate((6, 7)):
             o_ps = bank(b, [P, HALF])

@@ -14,6 +14,10 @@ U16 = mybir.dt.uint16
 U8 = mybir.dt.uint8
 FP8X4 = mybir.dt.float8_e4m3fn_x4
 MULT = mybir.AluOpType.mult
+MAX = mybir.AluOpType.max
+IS_GE = mybir.AluOpType.is_ge
+SUBTRACT = mybir.AluOpType.subtract
+AXIS_X = mybir.AxisListType.X
 COPY = mybir.ActivationFunctionType.Copy
 SQUARE = mybir.ActivationFunctionType.Square
 ABS = mybir.ActivationFunctionType.Abs
@@ -24,12 +28,11 @@ P = 128
 PACK = 4
 HALF = S // 2
 LIST_ROWS = 16
-TERMS = 3
-LAST_PLANE = PACK - 1
+BATCHES = S // P
 TINY = 2.0**-110
+PIVOT_SHARE = 2.0**-40
+PIVOT_FLOOR = 2.0**-100
 GPSIMD_CLEARS = 640
-WHOLE_PLANES = 2
-SUM_BANKS = (2, 3, 4, 5)
 
 
 def tile_picked_ace8_none_p_kernel(
@@ -43,66 +46,93 @@ def tile_picked_ace8_none_p_kernel(
         def bank(b, shape):
             return psum.tile(shape, F32, name=f"bank{b}", tag=f"bank{b}")
 
+        def sb(name, shape, dtype, tag=None):
+            return keep.tile(shape, dtype, name=name, tag=tag or name, align_bytes=64)
+
         def load_list(name, src):
             lt = keep.tile([P, S // LIST_ROWS], U16, name=name)
             nc.sync.dma_start(lt[:], src)
             return lt
-
-        def load_gain(name, src):
-            gt = keep.tile([P, S], F32, name=name, tag=name, align_bytes=64)
-            nc.sync.dma_start(gt[:], src)
-            return gt
-
-        def load_rows(name, src):
-            wr = keep.tile([P, PACK, src.shape[1]], F32, name=name, tag=name, align_bytes=64)
-            nc.sync.dma_start(wr[:], src.rearrange("(p j) c -> p j c", j=PACK))
-            return wr
 
         def load_factor(name, src):
             ct = keep.tile([P, PACK], F32, name=name)
             nc.sync.dma_start(ct[:], src.rearrange("(p t) o -> p (t o)", t=PACK))
             return ct
 
-        xs = keep.tile([P, T], U8, name="xs", tag="xs", align_bytes=64)
+        gains = sb("gains", [P, P], F32)
+        for src, lo, hi in ((g1, 0, 64), (g2, 64, 96), (g3, 96, 128)):
+            nc.scalar.dma_start(gains[lo:hi, :], src.rearrange("r (b c) -> (r b) c", c=P)[0 : hi - lo, :])
+        xs = sb("xs", [P, T], U8)
         nc.gpsimd.memset(xs[:, 0:GPSIMD_CLEARS].bitcast(I32), 0)
         nc.vector.memset(xs[:, GPSIMD_CLEARS:T].bitcast(I32), 0)
         offs_t = load_list("offs_t", offs)
         c2_t = load_factor("c2_t", c2)
-        w1_raw = load_rows("w1_raw", w1)
+        c1_t = load_factor("c1_t", c1)
+        w1_raw = sb("w1_raw", [P, PACK, H], F32)
+        nc.sync.dma_start(w1_raw[:], w1.rearrange("(p j) c -> p j c", j=PACK))
         for q in range(4):
             nc.sync.dma_start(
                 xs[32 * q : 32 * q + 4, :].bitcast(I32), x_scales[0, 4 * q : 4 * q + 4, :].bitcast(I32)
             )
-        xw = keep.tile([P, T], I32, name="xw", tag="xw", align_bytes=64)
+        xw = sb("xw", [P, T], I32)
         nc.sync.dma_start(xw[:], x_words[0].rearrange("p n t -> p (n t)").bitcast(I32))
-        c1_t = load_factor("c1_t", c1)
-        lists, gains = [], []
-        for k, (list_k, gain_k) in enumerate(((p1, g1), (p2, g2), (p3, g3))):
-            lists.append(load_list(f"list{k}", list_k))
-            gains.append(load_gain(f"gain{k}", gain_k))
-        w2_raw = load_rows("w2_raw", w2)
-        w3_raw = load_rows("w3_raw", w3)
+        w3_rows = w3.rearrange("(p j) c -> p j c", j=PACK)
+        w3_raw = [sb(f"w3_raw{i}", [P, PACK, HALF], F32) for i in range(2)]
+        nc.sync.dma_start(w3_raw[0][:], w3_rows[:, :, 0:HALF])
+        lists = [load_list(f"list{k}", src) for k, src in enumerate((p1, p2, p3))]
+        nc.sync.dma_start(w3_raw[1][:], w3_rows[:, :, HALF:N])
+        w2_rows = w2.rearrange("(p j) c -> p j c", j=PACK)
+        w2_raw = [sb(f"w2_raw{i}", [P, PACK, HALF], F32) for i in range(2)]
+        for i in range(2):
+            nc.sync.dma_start(w2_raw[i][:], w2_rows[:, :, i * HALF : (i + 1) * HALF])
 
         ident = keep.tile([P, P], F32, name="ident")
         make_identity(nc, ident[:])
 
-        mag, root, sign, inv_root, ratio = (
-            keep.tile([P, PACK], F32, name=name, tag=name, align_bytes=64)
-            for name in ("mag", "root", "sign", "inv_root", "ratio")
+        mag, root, not_below, sign, inv_root = (
+            sb(name, [P, PACK], F32) for name in ("mag", "root", "not_below", "sign", "inv_root")
         )
-        nc.scalar.activation(mag[:], c2_t[:], ABS)
+        nc.vector.scalar_tensor_tensor(mag[:], c2_t[:], -1.0, c2_t[:], MULT, MAX)
         nc.scalar.activation(root[:], mag[:], SQRT, bias=TINY)
-        nc.scalar.activation(sign[:], c2_t[:], SIGN, bias=TINY)
+        nc.vector.tensor_scalar(not_below[:], c2_t[:], 0.0, 2.0, IS_GE, MULT)
+        nc.vector.tensor_scalar(sign[:], not_below[:], 1.0, None, SUBTRACT)
         nc.vector.reciprocal(inv_root[:], root[:])
+        ratio = [sb(f"ratio{n}", [P, PACK], F32) for n in range(2)]
+        for n in range(2):
+            nc.vector.tensor_tensor(ratio[n][:], c1_t[:], inv_root[:], MULT)
 
-        w1_b = keep.tile([P, PACK, P, PACK], BF16, name="w1_b", align_bytes=64)
+        gains_ps = bank(0, [P, P])
+        nc.tensor.transpose(gains_ps[:], gains[:], ident[:])
+        g_cols = gains_ps[:, 32:P].rearrange("p (k q) -> p k q", q=32)[:, :, 0:BATCHES]
+        twice = sb("twice", [P, 3, BATCHES], F32)
+        half_sign, top, held, pivot, inv_pivot = (
+            sb(name, [P, BATCHES], F32) for name in ("half_sign", "top", "held", "pivot", "inv_pivot")
+        )
+        quot = sb("quot", [P, 2, BATCHES], F32)
+        nc.scalar.activation(twice[:], g_cols, ABS, scale=2.0)
+        nc.vector.tensor_scalar(half_sign[:], g_cols[:, 0, :], 0.0, 0.5, IS_GE, SUBTRACT)
+        nc.vector.tensor_reduce(top[:], twice[:].rearrange("p k b -> p b k"), AXIS_X, MAX)
+        nc.vector.scalar_tensor_tensor(held[:], top[:], PIVOT_SHARE, twice[:, 0, :], MULT, MAX)
+        nc.vector.scalar_tensor_tensor(pivot[:], held[:], PIVOT_FLOOR, half_sign[:], MAX, MULT)
+        nc.vector.reciprocal(inv_pivot[:], pivot[:])
+        nc.vector.tensor_tensor(
+            quot[:], g_cols[:, 1:3, :], inv_pivot[:].unsqueeze(1).to_broadcast([P, 2, BATCHES]), MULT
+        )
+        rows_ps = [bank(6 + k, [P, S]) for k in range(2)]
+        for k in range(2):
+            for b in range(BATCHES):
+                nc.tensor.transpose(
+                    rows_ps[k][:, b * P : (b + 1) * P], quot[:, k, b : b + 1].to_broadcast([P, P]), ident[:]
+                )
+
+        w1_b = sb("w1_b", [P, PACK, P, PACK], BF16, "gains")
         w1_q = []
-        w1_s = keep.tile([P, H], U8, name="w1_s", align_bytes=64)
+        w1_s = sb("w1_s", [P, H], U8)
         w1_from = w1_raw[:].rearrange("p j (m t) -> p m t j", t=PACK)
         w1_to = w1_b[:].rearrange("p t m j -> p m t j")
 
         def quantize_w1(pair, tag):
-            w1_q.append(keep.tile([P, 2 * P], U32, name=f"w1_q{pair}", tag=tag, align_bytes=64))
+            w1_q.append(sb(f"w1_q{pair}", [P, 2 * P], U32, tag))
             nc.vector.quantize_mx(
                 out=w1_q[pair][:].bitcast(FP8X4),
                 scales=w1_s[:, 2 * pair * P : 2 * (pair + 1) * P],
@@ -111,10 +141,13 @@ def tile_picked_ace8_none_p_kernel(
 
         for pair in range(2):
             nc.scalar.copy(w1_to[:, :, 2 * pair : 2 * pair + 2, :], w1_from[:, :, 2 * pair : 2 * pair + 2, :])
-        xs_g = keep.tile([P, S], U8, name="xs_g", align_bytes=64)
+        rows = sb("rows", [P, 2, S], F32, "w1_raw")
+        for k in range(2):
+            nc.scalar.copy(rows[:, k, :], rows_ps[k][:])
+        xs_g = sb("xs_g", [P, S], U8, "inv_pivot")
         nc.vector.tensor_copy(xs_g[:], xs[:].indirect(offs_t[:]))
         quantize_w1(0, "xs")
-        xw_g = [keep.tile([P, HALF], U32, name=f"xw_g{h}", align_bytes=64) for h in range(2)]
+        xw_g = [sb(f"xw_g{h}", [P, HALF], U32) for h in range(2)]
         for h in range(2):
             nc.vector.tensor_copy(
                 xw_g[h][:],
@@ -133,178 +166,166 @@ def tile_picked_ace8_none_p_kernel(
                 stop=True,
             )
 
-        y = []
+        y = [sb(f"y{t}", [P, 2 * S], F32) for t in range(PACK)]
         for t in range(PACK):
-            wide = t < WHOLE_PLANES
-            y.append(keep.tile([P, 2 * S if wide else S], F32, name=f"y{t}", align_bytes=64))
-            if wide:
-                nc.gpsimd.memset(y[t][:, S : 2 * S], 0.0)
-        for t in range(PACK):
-            nc.scalar.activation(ratio[:, t : t + 1], c1_t[:, t : t + 1], COPY, scale=inv_root[:, t : t + 1])
+            nc.gpsimd.memset(y[t][:, S : 2 * S], 0.0)
         for b, lo, width in ((0, 0, HALF), (1, HALF, P), (3, HALF + P, P)):
             ps = bank(b, [P, width])
             first_product(ps[:], 0, lo, width)
             nc.scalar.activation(y[0][:, lo : lo + width], ps[:], COPY, scale=root[:, 0:1])
-        for t, b in zip(range(1, PACK), (6, 7, 2)):
-            ps = bank(b, [P, S])
+        y_ps = {}
+        for t, b in zip(range(1, PACK), (4, 5, 2)):
+            y_ps[t] = bank(b, [P, S])
             for lo in (HALF, 0):
-                first_product(ps[:, lo : lo + HALF], t, lo, HALF)
-            nc.scalar.activation(y[t][:, 0:S], ps[:], COPY, scale=root[:, t : t + 1])
+                first_product(y_ps[t][:, lo : lo + HALF], t, lo, HALF)
 
-        w_b = [keep.tile([P, N, PACK], BF16, name=f"w_b{i}", align_bytes=64) for i in range(2)]
-        w_s = [keep.tile([P, N], U8, name=f"w_s{i}", align_bytes=64) for i in range(2)]
-        w3_signed = keep.tile([P, PACK, N], BF16, name="w3_signed")
+        def empty_plane(t):
+            nc.scalar.activation(y[t][:, 0:S], y_ps[t][:], COPY, scale=root[:, t : t + 1])
 
-        def weave(dst, rows):
+        w_q = {}
+        w_s = [sb(f"w_s{i}", [P, N], U8) for i in range(2)]
+        w3_b = sb("w3_b", [P, N, PACK], BF16, "gains")
+        w2_b = {}
+
+        def weave_w2(h, tag):
+            w2_b[h] = sb(f"w2_b{h}", [P, HALF, PACK], BF16, tag)
             nc.scalar.copy(
-                dst.rearrange("p (c i) t -> p c t i", i=4), rows.rearrange("p t (c i) -> p c t i", i=4)
+                w2_b[h][:].rearrange("p (c i) t -> p c t i", i=4), w2_raw[h][:].rearrange("p t (c i) -> p c t i", i=4)
             )
 
-        def weave_weights(i, rows, quarter):
-            cols = slice(quarter * P, (quarter + 1) * P)
-            weave(w_b[i][:, cols, :], rows[:, :, cols])
+        def weave_w3(h):
+            nc.vector.tensor_tensor(
+                w3_b[:, h * HALF : (h + 1) * HALF, :].rearrange("p (c i) t -> p c t i", i=4),
+                w3_raw[h][:].rearrange("p t (c i) -> p c t i", i=4),
+                sign[:].unsqueeze(1).unsqueeze(3).to_broadcast([P, HALF // 4, PACK, 4]), MULT,
+            )
 
-        def sign_rows(t):
-            nc.scalar.activation(w3_signed[:, t, :], w3_raw[:, t, :], COPY, scale=sign[:, t : t + 1])
+        def quantize_weights(i, woven, lo):
+            cols = slice(lo, lo + woven.shape[1])
+            nc.vector.quantize_mx(
+                out=w_q[i][:, cols].bitcast(FP8X4), scales=w_s[i][:, cols], in_=woven[:].rearrange("p m t -> p (m t)")
+            )
 
-        half_terms = []
+        def offsets(k, lo, width):
+            return lists[k][:, lo // LIST_ROWS : (lo + width) // LIST_ROWS]
 
-        def term_buffer(t, first, n):
-            if t < WHOLE_PLANES:
-                number = TERMS * t + n
-                slot = number if number <= TERMS else 2 + number % 2
-                return keep.tile([P, S], F32, name="term", tag=f"term{slot}", align_bytes=64)[:]
-            if (t, first, n) == (LAST_PLANE, 2, TERMS - 1):
-                return keep.tile([P, HALF], F32, name="term", tag="term3", align_bytes=64)[:]
-            if not half_terms:
-                half_terms.append(
-                    keep.tile([P, 2, 2, TERMS, HALF], F32, name="half_terms", tag="term2", align_bytes=64)
-                )
-            return half_terms[0][:, t - WHOLE_PLANES, first // 2, n, :]
+        def plain_term(dst, t, lo):
+            nc.scalar.activation(dst, y[t][:].indirect(offsets(0, lo, dst.shape[1])), COPY)
 
-        def sum_unit(t, first, batches, add_bank, turned_tag):
-            lo, width = first * P, batches * P
-            per_copy = 1 if t == LAST_PLANE else batches
-            turned_ps = bank(add_bank, [P, batches, P])
-            order = (2, 0, 1) if t == 1 else range(TERMS)
-            for n, k in enumerate(order):
-                term = term_buffer(t, first, n)
-                nc.vector.tensor_tensor(
-                    term,
-                    y[t][:].indirect(lists[k][:, lo // LIST_ROWS : (lo + width) // LIST_ROWS]),
-                    gains[k][:, lo : lo + width],
-                    MULT,
-                )
-                for b in range(batches):
-                    nc.tensor.matmul(
-                        turned_ps[:, b, :], term[:, b * P : (b + 1) * P], ident[:],
-                        start=(n == 0 and b == 0), stop=(n == TERMS - 1 and b == batches - 1), is_transpose=True,
-                    )
-            turned = keep.tile([P, batches, P], F32, name="turned", tag=turned_tag, align_bytes=64)
-            for piece in range(0, batches, per_copy):
-                nc.scalar.copy(turned[:, piece : piece + per_copy, :], turned_ps[:, piece : piece + per_copy, :])
-                for b in range(piece, piece + per_copy):
-                    nc.tensor.transpose(sums[first + b][:, :, t], turned[:, b, :], ident[:])
+        def scaled_term(dst, t, k, lo):
+            width = dst.shape[1]
+            nc.vector.tensor_tensor(
+                dst, y[t][:].indirect(offsets(k, lo, width)), rows[:, k - 1, lo : lo + width], MULT
+            )
+
+        def turn_back(ps, plane, which, first, turned=None):
+            planes = ps.shape[2]
+            if turned is None:
+                turned = sb(f"turned{plane}_{first}", [P, len(which), planes, P], F32)[:]
+            for n, i in enumerate(which):
+                b = first + i
+                nc.scalar.activation(turned[:, n], ps[:, i], COPY, scale=pivot[:, b : b + 1])
+                for slot in range(planes):
+                    nc.tensor.transpose(sums[b][:, plane + slot, :], turned[:, n, slot, :], ident[:])
 
         def first_order(dst, b):
-            nc.vector.tensor_tensor(dst, sums[b][:], ratio[:].unsqueeze(1).to_broadcast([P, P, PACK]), MULT)
+            nc.vector.tensor_tensor(
+                dst, sums[b][:].rearrange("p t j -> p j t"),
+                ratio[0 if b == 1 else 1][:].unsqueeze(1).to_broadcast([P, P, PACK]), MULT,
+            )
 
         def second_order(dst, b):
-            nc.scalar.activation(dst, sums[b][:], SQUARE)
+            nc.scalar.activation(dst, sums[b][:].rearrange("p t j -> p j t"), SQUARE)
 
-        sums = [bank(b, [P, P, PACK]) for b in SUM_BANKS]
-        values_a = keep.tile([P, 2, HALF, PACK], BF16, name="values_a", align_bytes=64)
-        values_b = [keep.tile([P, 2, P, PACK], BF16, name=f"values_b{b}", align_bytes=64) for b in range(2)]
-        z2_planes = keep.tile([P, PACK, P], BF16, name="z2_planes", align_bytes=64)
-
-        def z2_plane(t):
-            nc.scalar.activation(z2_planes[:, t, :], sums[0][:, :, t], COPY, scale=ratio[:, t : t + 1])
-
-        for q in range(PACK):
-            weave_weights(0, w2_raw, q)
-        for t in range(PACK):
-            sign_rows(t)
-        sum_unit(0, 0, 4, 0, "w2_raw")
-        for q in range(2):
-            weave_weights(1, w3_signed, q)
-        sum_unit(1, 0, 4, 1, "w3_raw")
-        for q in range(2, PACK):
-            weave_weights(1, w3_signed, q)
-        sum_unit(2, 0, 2, 0, "sign")
-        z2_plane(0)
-        z2_plane(1)
-        sum_unit(3, 0, 2, 1, "turned_a3")
-        z2_plane(2)
-        z2_plane(3)
-        second_order(values_a[:, 1, 0:P, :], 0)
-        sum_unit(2, 2, 2, 1, "turned_b2")
-        second_order(values_a[:, 1, P:HALF, :], 1)
-        weave(values_a[:, 0, 0:P, :], z2_planes[:])
-        sum_unit(3, 2, 2, SUM_BANKS[0], "turned_b3")
-        first_order(values_a[:, 0, P:HALF, :], 1)
-
-        codes = keep.tile([P, 3, N], U32, name="codes", tag="term2", align_bytes=64)
-        out_v = out.rearrange("(a p) j -> p a j", p=P)
-
-        def quantize_weights(i):
+        def quantize_values(name, values):
+            width = 2 * values.shape[2]
+            zq = sb(f"zq{name}", [P, width], U32)
+            zs = sb(f"zs{name}", [P, width], U8)
             nc.vector.quantize_mx(
-                out=codes[:, i, :].bitcast(FP8X4), scales=w_s[i][:], in_=w_b[i][:].rearrange("p m t -> p (m t)")
+                out=zq[:].bitcast(FP8X4), scales=zs[:], in_=values[:].rearrange("p o j t -> p (o j t)")
             )
+            return zq, zs
 
-        def quantize_values(name, values, zq):
-            zs = keep.tile([P, 2 * values.shape[2]], U8, name=f"zs{name}", align_bytes=64)
-            nc.vector.quantize_mx(
-                out=zq.bitcast(FP8X4), scales=zs[:], in_=values[:].rearrange("p o j t -> p (o j t)")
-            )
-            return zs
-
-        def last_pass(o_ps, i, tile_number, zq, zs, start, stop):
+        def output_tile(o_ps, a, z):
             width = o_ps.shape[1]
-            rows = slice(tile_number * P, (tile_number + 1) * P)
-            nc.tensor.matmul_mx(
-                out=o_ps,
-                lhsT=codes[:, i, rows].bitcast(FP8X4),
-                lhsT_scale=w_s[i][:, rows],
-                rhs=zq[:, i * width : (i + 1) * width].bitcast(FP8X4),
-                rhs_scale=zs[:, i * width : (i + 1) * width],
-                start=start,
-                stop=stop,
-            )
+            for i in range(2):
+                nc.tensor.matmul_mx(
+                    out=o_ps,
+                    lhsT=w_q[i][:, a * P : (a + 1) * P].bitcast(FP8X4),
+                    lhsT_scale=w_s[i][:, a * P : (a + 1) * P],
+                    rhs=z[0][:, i * width : (i + 1) * width].bitcast(FP8X4),
+                    rhs_scale=z[1][:, i * width : (i + 1) * width],
+                    start=i == 0,
+                    stop=i == 1,
+                )
 
-        quantize_weights(0)
-        zq_a = codes[:, 2, :]
-        zs_a = quantize_values("a", values_a, zq_a)
-        quantize_weights(1)
+        out_v = out.rearrange("(a p) j -> p a j", p=P)
+        sums = {}
+        values_a = sb("values_a", [P, 2, HALF, PACK], BF16)
+        values_b = [sb(f"values_b{b}", [P, 2, P, PACK], BF16) for b in range(2)]
+
+        plain = [sb(f"plain{t}", [P, S], F32) for t in range(PACK)]
+
+        def unit(t, lo, width, groups):
+            scaled = sb(f"scaled{t}_{lo}", [P, 2, width], F32)
+            for k in (1, 2):
+                scaled_term(scaled[:, k - 1, :], t, k, lo)
+            for n, term in enumerate((plain[t][:, lo : lo + width], scaled[:, 0, :], scaled[:, 1, :])):
+                for i in range(width // P):
+                    nc.tensor.matmul(
+                        groups[i // 2][:, i % 2, t % 2, :], term[:, i * P : (i + 1) * P], ident[:],
+                        start=(t % 2, n, i % 2) == (0, 0, 0), stop=(t % 2, n, i % 2) == (1, 2, 1), is_transpose=True,
+                    )
+
+        for t in range(PACK):
+            if t + 1 < PACK:
+                empty_plane(t + 1)
+            plain_term(plain[t][:], t, 0)
+        low = [bank(h, [P, 2, 2, P]) for h in range(2)]
+        weave_w3(0)
+        unit(0, 0, S, low)
+        weave_w3(1)
+        unit(1, 0, S, low)
+        for b in range(BATCHES):
+            sums[b] = bank(2 + b, [P, PACK, P])
+        for h in range(2):
+            turn_back(low[h], 0, (0, 1), 2 * h)
+        weave_w2(0, "scaled1_0")
+        high = [bank(6 + h, [P, 2, 2, P]) for h in range(2)]
+        for t in (2, 3):
+            unit(t, 0, HALF, high[0:1])
+        unit(2, HALF, HALF, high[1:2])
+        turn_back(high[0], 2, (0, 1), 0, sb("turned_a", [P, 2, 2, P], F32, "w2_raw0")[:])
+        unit(3, HALF, HALF, high[1:2])
+        weave_w2(1, "scaled3_0")
+        w_q[0] = sb("w2_q", [P, N], U32, "y3")
+        second_order(values_a[:, 1, 0:P, :], 0)
+        first_order(values_a[:, 0, P:HALF, :], 1)
+        for h in range(2):
+            quantize_weights(0, w2_b[h], h * HALF)
+        second_order(values_a[:, 1, P:HALF, :], 1)
+        first_order(values_a[:, 0, 0:P, :], 0)
+        turn_back(high[1], 2, (0, 1), 2, sb("turned_b", [P, 2, 2, P], F32, "w2_raw1")[:])
+        w_q[1] = sb("w3_q", [P, N], U32, "ratio0")
+        quantize_weights(1, w3_b, 0)
+        z_a = quantize_values("a", values_a)
         for b in range(2):
             second_order(values_b[b][:, 1], 2 + b)
-        for b in range(2):
             first_order(values_b[b][:, 0], 2 + b)
-
-        o_ps = bank(SUM_BANKS[0], [P, 2, HALF])
-        for i in range(2):
+        out_a = [bank(pair, [P, 2, HALF]) for pair in range(2)]
+        for pair in range(2):
             for a in range(2):
-                last_pass(o_ps[:, a, :], i, a, zq_a, zs_a, (i, a) == (0, 0), (i, a) == (1, 1))
-        for a in range(2):
-            o_sb = keep.tile([P, HALF], F32, name=f"o_sba0_{a}")
-            nc.scalar.copy(o_sb[:], o_ps[:, a, :])
-            nc.sync.dma_start(out_v[:, a, 0:HALF], o_sb[:])
-        o_sb = keep.tile([P, 2, HALF], F32, name="o_sba1")
-        for a, b in enumerate((6, 7)):
-            o_ps = bank(b, [P, HALF])
-            for i in (1, 0):
-                last_pass(o_ps[:], i, 2 + a, zq_a, zs_a, i == 1, i == 0)
-            nc.scalar.copy(o_sb[:, a, :], o_ps[:])
-        nc.sync.dma_start(out_v[:, 2:4, 0:HALF], o_sb[:])
-
-        for b, banks in enumerate(((0, 1), SUM_BANKS[2:])):
-            zq_b = keep.tile([P, 2 * P], U32, name=f"zq_b{b}", align_bytes=64)
-            zs_b = quantize_values(f"b{b}", values_b[b], zq_b[:])
+                output_tile(out_a[pair][:, a, :], 2 * pair + a, z_a)
+            o_sb = sb(f"o_a{pair}", [P, 2, HALF], F32)
+            nc.scalar.copy(o_sb[:], out_a[pair][:])
+            nc.sync.dma_start(out_v[:, 2 * pair : 2 * pair + 2, 0:HALF], o_sb[:])
+        for b, banks in enumerate(((6, 7), (2, 3))):
+            z_b = quantize_values(f"b{b}", values_b[b])
             for pair, copy in enumerate((nc.scalar.copy, nc.vector.tensor_copy)):
                 o_ps = bank(banks[pair], [P, 2, P])
                 for a in range(2):
-                    for i in range(2):
-                        last_pass(o_ps[:, a, :], i, 2 * pair + a, zq_b[:], zs_b, i == 0, i == 1)
-                o_sb = keep.tile([P, 2, P], F32, name=f"o_sbb{b}_{pair}")
+                    output_tile(o_ps[:, a, :], 2 * pair + a, z_b)
+                o_sb = sb(f"o_b{b}_{pair}", [P, 2, P], F32)
                 copy(o_sb[:], o_ps[:])
                 first = HALF + b * P
                 nc.sync.dma_start(out_v[:, 2 * pair : 2 * pair + 2, first : first + P], o_sb[:])

@@ -97,9 +97,8 @@ def tile_picked_ace8_none_p_kernel(
         nc.vector.tensor_scalar(not_below[:], c2_t[:], 0.0, 2.0, IS_GE, MULT)
         nc.vector.tensor_scalar(sign[:], not_below[:], 1.0, None, SUBTRACT)
         nc.vector.reciprocal(inv_root[:], root[:])
-        ratio = [sb(f"ratio{n}", [P, PACK], F32) for n in range(2)]
-        for n in range(2):
-            nc.vector.tensor_tensor(ratio[n][:], c1_t[:], inv_root[:], MULT)
+        ratio = sb("ratio", [P, PACK], F32)
+        nc.vector.tensor_tensor(ratio[:], c1_t[:], inv_root[:], MULT)
 
         gains_ps = bank(0, [P, P])
         nc.tensor.transpose(gains_ps[:], gains[:], ident[:])
@@ -231,37 +230,35 @@ def tile_picked_ace8_none_p_kernel(
         def first_order(dst, b):
             nc.vector.tensor_tensor(
                 dst, sums[b][:].rearrange("p t j -> p j t"),
-                ratio[0 if b == 1 else 1][:].unsqueeze(1).to_broadcast([P, P, PACK]), MULT,
+                ratio[:].unsqueeze(1).to_broadcast([P, P, PACK]), MULT,
             )
 
         def second_order(dst, b):
             nc.scalar.activation(dst, sums[b][:].rearrange("p t j -> p j t"), SQUARE)
 
         def quantize_values(name, values):
-            width = 2 * values.shape[2]
+            width = values.shape[1] // PACK
             zq = sb(f"zq{name}", [P, width], U32)
             zs = sb(f"zs{name}", [P, width], U8)
-            nc.vector.quantize_mx(
-                out=zq[:].bitcast(FP8X4), scales=zs[:], in_=values[:].rearrange("p o j t -> p (o j t)")
-            )
+            nc.vector.quantize_mx(out=zq[:].bitcast(FP8X4), scales=zs[:], in_=values)
             return zq, zs
 
-        def output_tile(o_ps, a, z):
+        def one_pass(o_ps, i, a, z, lo, start, stop):
             width = o_ps.shape[1]
-            for i in range(2):
-                nc.tensor.matmul_mx(
-                    out=o_ps,
-                    lhsT=w_q[i][:, a * P : (a + 1) * P].bitcast(FP8X4),
-                    lhsT_scale=w_s[i][:, a * P : (a + 1) * P],
-                    rhs=z[0][:, i * width : (i + 1) * width].bitcast(FP8X4),
-                    rhs_scale=z[1][:, i * width : (i + 1) * width],
-                    start=i == 0,
-                    stop=i == 1,
-                )
+            nc.tensor.matmul_mx(
+                out=o_ps,
+                lhsT=w_q[i][:, a * P : (a + 1) * P].bitcast(FP8X4),
+                lhsT_scale=w_s[i][:, a * P : (a + 1) * P],
+                rhs=z[0][:, lo : lo + width].bitcast(FP8X4),
+                rhs_scale=z[1][:, lo : lo + width],
+                start=start,
+                stop=stop,
+            )
 
         out_v = out.rearrange("(a p) j -> p a j", p=P)
         sums = {}
-        values_a = sb("values_a", [P, 2, HALF, PACK], BF16)
+        squares_a = sb("squares_a", [P, HALF, PACK], BF16)
+        products_a = sb("products_a", [P, HALF, PACK], BF16)
         values_b = [sb(f"values_b{b}", [P, 2, P, PACK], BF16) for b in range(2)]
 
         plain = [sb(f"plain{t}", [P, S], F32) for t in range(PACK)]
@@ -298,33 +295,37 @@ def tile_picked_ace8_none_p_kernel(
         turn_back(high[0], 2, (0, 1), 0, sb("turned_a", [P, 2, 2, P], F32, "w2_raw0")[:])
         unit(3, HALF, HALF, high[1:2])
         weave_w2(1, "scaled3_0")
-        w_q[0] = sb("w2_q", [P, N], U32, "y3")
-        second_order(values_a[:, 1, 0:P, :], 0)
-        first_order(values_a[:, 0, P:HALF, :], 1)
-        for h in range(2):
-            quantize_weights(0, w2_b[h], h * HALF)
-        second_order(values_a[:, 1, P:HALF, :], 1)
-        first_order(values_a[:, 0, 0:P, :], 0)
+        codes = sb("codes", [P, 2, N], U32, "y3")
+        w_q[0], w_q[1] = codes[:, 0, :], codes[:, 1, :]
+        for b in range(2):
+            second_order(squares_a[:, b * P : (b + 1) * P, :], b)
         turn_back(high[1], 2, (0, 1), 2, sb("turned_b", [P, 2, 2, P], F32, "w2_raw1")[:])
-        w_q[1] = sb("w3_q", [P, N], U32, "ratio0")
         quantize_weights(1, w3_b, 0)
-        z_a = quantize_values("a", values_a)
+        quantize_weights(0, w2_b[0], 0)
+        first_order(products_a[:, 0:P, :], 0)
+        out_a = [bank(pair, [P, 2, HALF]) for pair in range(2)]
+        z_a = quantize_values("a1", squares_a[:].rearrange("p j t -> p (j t)"))
+        for a in range(4):
+            one_pass(out_a[a // 2][:, a % 2, :], 1, a, z_a, 0, a % 2 == 0, False)
+        first_order(products_a[:, P:HALF, :], 1)
+        quantize_weights(0, w2_b[1], HALF)
+        z_a = quantize_values("a0", products_a[:].rearrange("p j t -> p (j t)"))
         for b in range(2):
             second_order(values_b[b][:, 1], 2 + b)
             first_order(values_b[b][:, 0], 2 + b)
-        out_a = [bank(pair, [P, 2, HALF]) for pair in range(2)]
         for pair in range(2):
             for a in range(2):
-                output_tile(out_a[pair][:, a, :], 2 * pair + a, z_a)
+                one_pass(out_a[pair][:, a, :], 0, 2 * pair + a, z_a, 0, False, a == 1)
             o_sb = sb(f"o_a{pair}", [P, 2, HALF], F32)
             nc.scalar.copy(o_sb[:], out_a[pair][:])
             nc.sync.dma_start(out_v[:, 2 * pair : 2 * pair + 2, 0:HALF], o_sb[:])
         for b, banks in enumerate(((6, 7), (2, 3))):
-            z_b = quantize_values(f"b{b}", values_b[b])
+            z_b = quantize_values(f"b{b}", values_b[b][:].rearrange("p o j t -> p (o j t)"))
             for pair, copy in enumerate((nc.scalar.copy, nc.vector.tensor_copy)):
                 o_ps = bank(banks[pair], [P, 2, P])
                 for a in range(2):
-                    output_tile(o_ps[:, a, :], 2 * pair + a, z_b)
+                    for i in range(2):
+                        one_pass(o_ps[:, a, :], i, 2 * pair + a, z_b, i * P, i == 0, i == 1)
                 o_sb = sb(f"o_b{b}_{pair}", [P, 2, P], F32)
                 copy(o_sb[:], o_ps[:])
                 first = HALF + b * P

@@ -225,16 +225,16 @@ def tile_picked_ace8_none_p_kernel(
                 b = first + i
                 nc.scalar.activation(turned[:, n], ps[:, i], COPY, scale=pivot[:, b : b + 1])
                 for slot in range(planes):
-                    nc.tensor.transpose(sums[b][:, plane + slot, :], turned[:, n, slot, :], ident[:])
+                    nc.tensor.transpose(sums[b][:, :, plane + slot], turned[:, n, slot, :], ident[:])
 
         def first_order(dst, b):
             nc.vector.tensor_tensor(
-                dst, sums[b][:].rearrange("p t j -> p j t"),
+                dst, sums[b][:],
                 ratio[:].unsqueeze(1).to_broadcast([P, P, PACK]), MULT,
             )
 
         def second_order(dst, b):
-            nc.scalar.activation(dst, sums[b][:].rearrange("p t j -> p j t"), SQUARE)
+            nc.scalar.activation(dst, sums[b][:], SQUARE)
 
         def quantize_values(name, values):
             width = values.shape[1] // PACK
@@ -284,7 +284,7 @@ def tile_picked_ace8_none_p_kernel(
         weave_w3(1)
         unit(1, 0, S, low)
         for b in range(BATCHES):
-            sums[b] = bank(2 + b, [P, PACK, P])
+            sums[b] = bank(2 + b, [P, P, PACK])
         for h in range(2):
             turn_back(low[h], 0, (0, 1), 2 * h)
         weave_w2(0, "scaled1_0")

@@ -70,10 +70,8 @@ def tile_picked_ace8_none_p_kernel(
         c1_t = load_factor("c1_t", c1)
         w1_raw = sb("w1_raw", [P, PACK, H], F32)
         nc.sync.dma_start(w1_raw[:], w1.rearrange("(p j) c -> p j c", j=PACK))
-        for q in range(4):
-            nc.sync.dma_start(
-                xs[32 * q : 32 * q + 4, :].bitcast(I32), x_scales[0, 4 * q : 4 * q + 4, :].bitcast(I32)
-            )
+        for i in range(4):
+            nc.sync.dma_start(xs[i:P:32, :].bitcast(I32), x_scales[0, i:16:4, :].bitcast(I32))
         xw = sb("xw", [P, T], I32)
         nc.sync.dma_start(xw[:], x_words[0].rearrange("p n t -> p (n t)").bitcast(I32))
         w3_rows = w3.rearrange("(p j) c -> p j c", j=PACK)
@@ -165,9 +163,9 @@ def tile_picked_ace8_none_p_kernel(
                 stop=True,
             )
 
-        y = [sb(f"y{t}", [P, 2 * S], F32) for t in range(PACK)]
-        for t in range(PACK):
-            nc.gpsimd.memset(y[t][:, S : 2 * S], 0.0)
+        y = [sb(f"y{t}", [P, 2 * S if t < 2 else S], F32) for t in range(PACK)]
+        for t in range(2):
+            nc.vector.memset(y[t][:, S : 2 * S].bitcast(I32), 0)
         for b, lo, width in ((0, 0, HALF), (1, HALF, P), (3, HALF + P, P)):
             ps = bank(b, [P, width])
             first_product(ps[:], 0, lo, width)
@@ -277,7 +275,9 @@ def tile_picked_ace8_none_p_kernel(
         for t in range(PACK):
             if t + 1 < PACK:
                 empty_plane(t + 1)
-            plain_term(plain[t][:], t, 0)
+            width = S if t < 2 else HALF
+            for lo in range(0, S, width):
+                plain_term(plain[t][:, lo : lo + width], t, lo)
         low = [bank(h, [P, 2, 2, P]) for h in range(2)]
         weave_w3(0)
         unit(0, 0, S, low)

@@ -200,7 +200,7 @@ def tile_picked_ace8_none_p_kernel(
         def quantize_weights(i, woven, lo):
             cols = slice(lo, lo + woven.shape[1])
             nc.vector.quantize_mx(
-                out=w_q[i][:, cols].bitcast(FP8X4), scales=w_s[i][:, cols], in_=woven[:].rearrange("p m t -> p (m t)")
+                out=w_q[i][:, cols].bitcast(FP8X4), scales=w_s[i][:, cols], in_=woven.rearrange("p m t -> p (m t)")
             )
 
         def offsets(k, lo, width):
@@ -257,38 +257,45 @@ def tile_picked_ace8_none_p_kernel(
         sums = {}
         squares_a = sb("squares_a", [P, HALF, PACK], BF16)
         products_a = sb("products_a", [P, HALF, PACK], BF16)
-        values_b = [sb(f"values_b{b}", [P, 2, P, PACK], BF16) for b in range(2)]
+        squares_b = sb("squares_b", [P, HALF, PACK], BF16)
+        products_b = [sb(f"products_b{b}", [P, P, PACK], BF16) for b in range(2)]
 
         plain = [sb(f"plain{t}", [P, S], F32) for t in range(PACK)]
+
+        def add_term(term, t, groups, start, stop):
+            for i in range(term.shape[1] // P):
+                nc.tensor.matmul(
+                    groups[i // 2][:, i % 2, t % 2, :], term[:, i * P : (i + 1) * P], ident[:],
+                    start=start and i % 2 == 0, stop=stop and i % 2 == 1, is_transpose=True,
+                )
 
         def unit(t, lo, width, groups):
             scaled = sb(f"scaled{t}_{lo}", [P, 2, width], F32)
             for k in (1, 2):
                 scaled_term(scaled[:, k - 1, :], t, k, lo)
-            for n, term in enumerate((plain[t][:, lo : lo + width], scaled[:, 0, :], scaled[:, 1, :])):
-                for i in range(width // P):
-                    nc.tensor.matmul(
-                        groups[i // 2][:, i % 2, t % 2, :], term[:, i * P : (i + 1) * P], ident[:],
-                        start=(t % 2, n, i % 2) == (0, 0, 0), stop=(t % 2, n, i % 2) == (1, 2, 1), is_transpose=True,
-                    )
+                add_term(scaled[:, k - 1, :], t, groups, False, t % 2 == 1 and k == 2)
 
+        low = [bank(h, [P, 2, 2, P]) for h in range(2)]
+        high = [bank(6 + h, [P, 2, 2, P]) for h in range(2)]
         for t in range(PACK):
             if t + 1 < PACK:
                 empty_plane(t + 1)
             width = S if t < 2 else HALF
             for lo in range(0, S, width):
                 plain_term(plain[t][:, lo : lo + width], t, lo)
-        low = [bank(h, [P, 2, 2, P]) for h in range(2)]
         weave_w3(0)
+        add_term(plain[0][:], 0, low, True, False)
         unit(0, 0, S, low)
         weave_w3(1)
+        add_term(plain[1][:], 1, low, False, False)
+        add_term(plain[2][:], 2, high, True, False)
         unit(1, 0, S, low)
+        add_term(plain[3][:], 3, high, False, False)
         for b in range(BATCHES):
             sums[b] = bank(2 + b, [P, P, PACK])
         for h in range(2):
             turn_back(low[h], 0, (0, 1), 2 * h)
         weave_w2(0, "scaled1_0")
-        high = [bank(6 + h, [P, 2, 2, P]) for h in range(2)]
         for t in (2, 3):
             unit(t, 0, HALF, high[0:1])
         unit(2, HALF, HALF, high[1:2])
@@ -300,33 +307,44 @@ def tile_picked_ace8_none_p_kernel(
         for b in range(2):
             second_order(squares_a[:, b * P : (b + 1) * P, :], b)
         turn_back(high[1], 2, (0, 1), 2, sb("turned_b", [P, 2, 2, P], F32, "w2_raw1")[:])
-        quantize_weights(1, w3_b, 0)
-        quantize_weights(0, w2_b[0], 0)
+        def leave(o_ps, first_tile, name):
+            o_sb = sb(name, list(o_ps.shape), F32)
+            nc.scalar.copy(o_sb[:], o_ps)
+            nc.sync.dma_start(out_v[:, first_tile : first_tile + o_ps.shape[1], 0:HALF], o_sb[:])
+
+        quantize_weights(1, w3_b[:, 0:HALF, :], 0)
         first_order(products_a[:, 0:P, :], 0)
-        out_a = [bank(pair, [P, 2, HALF]) for pair in range(2)]
-        z_a = quantize_values("a1", squares_a[:].rearrange("p j t -> p (j t)"))
-        for a in range(4):
-            one_pass(out_a[a // 2][:, a % 2, :], 1, a, z_a, 0, a % 2 == 0, False)
+        out_a = [bank(0, [P, 1, HALF]), bank(1, [P, 1, HALF]), bank(6, [P, 2, HALF])]
+        z_sq_a = quantize_values("a1", squares_a[:].rearrange("p j t -> p (j t)"))
+        for a in range(2):
+            one_pass(out_a[a][:, 0, :], 1, a, z_sq_a, 0, True, False)
         first_order(products_a[:, P:HALF, :], 1)
-        quantize_weights(0, w2_b[1], HALF)
+        quantize_weights(0, w2_b[0][:], 0)
         z_a = quantize_values("a0", products_a[:].rearrange("p j t -> p (j t)"))
         for b in range(2):
-            second_order(values_b[b][:, 1], 2 + b)
-            first_order(values_b[b][:, 0], 2 + b)
-        for pair in range(2):
+            second_order(squares_b[:, b * P : (b + 1) * P, :], 2 + b)
+        for a in range(2):
+            one_pass(out_a[a][:, 0, :], 0, a, z_a, 0, False, True)
+            leave(out_a[a][:], a, f"o_a{a}")
+        quantize_weights(1, w3_b[:, HALF:N, :], HALF)
+        quantize_weights(0, w2_b[1][:], HALF)
+        for i, z in ((1, z_sq_a), (0, z_a)):
             for a in range(2):
-                one_pass(out_a[pair][:, a, :], 0, 2 * pair + a, z_a, 0, False, a == 1)
-            o_sb = sb(f"o_a{pair}", [P, 2, HALF], F32)
-            nc.scalar.copy(o_sb[:], out_a[pair][:])
-            nc.sync.dma_start(out_v[:, 2 * pair : 2 * pair + 2, 0:HALF], o_sb[:])
-        for b, banks in enumerate(((6, 7), (2, 3))):
-            z_b = quantize_values(f"b{b}", values_b[b][:].rearrange("p o j t -> p (o j t)"))
+                one_pass(out_a[2][:, a, :], i, 2 + a, z, 0, (i, a) == (1, 0), (i, a) == (0, 1))
+        leave(out_a[2][:], 2, "o_a2")
+        first_order(products_b[0][:], 2)
+        z_sq = quantize_values("b_squares", squares_b[:].rearrange("p j t -> p (j t)"))
+        first_order(products_b[1][:], 3)
+        out_b = [[bank(n, [P, 2, P]) for n in banks] for banks in ((7, 2), (3, 0))]
+        for b in range(2):
+            for a in range(4):
+                one_pass(out_b[b][a // 2][:, a % 2, :], 1, a, z_sq, b * P, a % 2 == 0, False)
+        for b in range(2):
+            z_b = quantize_values(f"b{b}", products_b[b][:].rearrange("p j t -> p (j t)"))
             for pair, copy in enumerate((nc.scalar.copy, nc.vector.tensor_copy)):
-                o_ps = bank(banks[pair], [P, 2, P])
                 for a in range(2):
-                    for i in range(2):
-                        one_pass(o_ps[:, a, :], i, 2 * pair + a, z_b, i * P, i == 0, i == 1)
+                    one_pass(out_b[b][pair][:, a, :], 0, 2 * pair + a, z_b, 0, False, a == 1)
                 o_sb = sb(f"o_b{b}_{pair}", [P, 2, P], F32)
-                copy(o_sb[:], o_ps[:])
+                copy(o_sb[:], out_b[b][pair][:])
                 first = HALF + b * P
                 nc.sync.dma_start(out_v[:, 2 * pair : 2 * pair + 2, first : first + P], o_sb[:])

@@ -15,13 +15,11 @@ U8 = mybir.dt.uint8
 FP8X4 = mybir.dt.float8_e4m3fn_x4
 MULT = mybir.AluOpType.mult
 MAX = mybir.AluOpType.max
+MIN = mybir.AluOpType.min
 IS_GE = mybir.AluOpType.is_ge
 SUBTRACT = mybir.AluOpType.subtract
-AXIS_X = mybir.AxisListType.X
 COPY = mybir.ActivationFunctionType.Copy
 SQUARE = mybir.ActivationFunctionType.Square
-ABS = mybir.ActivationFunctionType.Abs
-SIGN = mybir.ActivationFunctionType.Sign
 SQRT = mybir.ActivationFunctionType.Sqrt
 
 P = 128
@@ -30,8 +28,7 @@ HALF = S // 2
 LIST_ROWS = 16
 BATCHES = S // P
 TINY = 2.0**-110
-PIVOT_SHARE = 2.0**-40
-PIVOT_FLOOR = 2.0**-100
+INV_BOUND = 2.0**63
 GPSIMD_CLEARS = 640
 
 
@@ -101,19 +98,14 @@ def tile_picked_ace8_none_p_kernel(
         gains_ps = bank(0, [P, P])
         nc.tensor.transpose(gains_ps[:], gains[:], ident[:])
         g_cols = gains_ps[:, 32:P].rearrange("p (k q) -> p k q", q=32)[:, :, 0:BATCHES]
-        twice = sb("twice", [P, 3, BATCHES], F32)
-        half_sign, top, held, pivot, inv_pivot = (
-            sb(name, [P, BATCHES], F32) for name in ("half_sign", "top", "held", "pivot", "inv_pivot")
-        )
-        quot = sb("quot", [P, 2, BATCHES], F32)
-        nc.scalar.activation(twice[:], g_cols, ABS, scale=2.0)
-        nc.vector.tensor_scalar(half_sign[:], g_cols[:, 0, :], 0.0, 0.5, IS_GE, SUBTRACT)
-        nc.vector.tensor_reduce(top[:], twice[:].rearrange("p k b -> p b k"), AXIS_X, MAX)
-        nc.vector.scalar_tensor_tensor(held[:], top[:], PIVOT_SHARE, twice[:, 0, :], MULT, MAX)
-        nc.vector.scalar_tensor_tensor(pivot[:], held[:], PIVOT_FLOOR, half_sign[:], MAX, MULT)
-        nc.vector.reciprocal(inv_pivot[:], pivot[:])
+        inv_gain, inv_pivot, pivot = (sb(name, [P, BATCHES], F32) for name in ("inv_gain", "inv_pivot", "pivot"))
+        others, quot = (sb(name, [P, 2, BATCHES], F32) for name in ("others", "quot"))
+        nc.vector.reciprocal(inv_gain[:], g_cols[:, 0, :])
+        nc.vector.tensor_copy(others[:], g_cols[:, 1:3, :])
+        nc.vector.tensor_scalar(inv_pivot[:], inv_gain[:], INV_BOUND, -INV_BOUND, MIN, MAX)
+        nc.vector.reciprocal(pivot[:], inv_pivot[:])
         nc.vector.tensor_tensor(
-            quot[:], g_cols[:, 1:3, :], inv_pivot[:].unsqueeze(1).to_broadcast([P, 2, BATCHES]), MULT
+            quot[:], others[:], inv_pivot[:].unsqueeze(1).to_broadcast([P, 2, BATCHES]), MULT
         )
         rows_ps = [bank(6 + k, [P, S]) for k in range(2)]
         for k in range(2):
@@ -122,42 +114,36 @@ def tile_picked_ace8_none_p_kernel(
                     rows_ps[k][:, b * P : (b + 1) * P], quot[:, k, b : b + 1].to_broadcast([P, P]), ident[:]
                 )
 
-        w1_b = sb("w1_b", [P, PACK, P, PACK], BF16, "gains")
-        w1_q = []
-        w1_s = sb("w1_s", [P, H], U8)
         w1_from = w1_raw[:].rearrange("p j (m t) -> p m t j", t=PACK)
-        w1_to = w1_b[:].rearrange("p t m j -> p m t j")
-
-        def quantize_w1(pair, tag):
-            w1_q.append(sb(f"w1_q{pair}", [P, 2 * P], U32, tag))
-            nc.vector.quantize_mx(
-                out=w1_q[pair][:].bitcast(FP8X4),
-                scales=w1_s[:, 2 * pair * P : 2 * (pair + 1) * P],
-                in_=w1_b[:, 2 * pair : 2 * pair + 2].rearrange("p t m j -> p (t m j)"),
-            )
-
-        for pair in range(2):
-            nc.scalar.copy(w1_to[:, :, 2 * pair : 2 * pair + 2, :], w1_from[:, :, 2 * pair : 2 * pair + 2, :])
+        w1_b = [sb(f"w1_b{pair}", [P, 2, P, PACK], BF16, tag) for pair, tag in enumerate(("gains", "inv_pivot"))]
+        for pair, copy in enumerate((nc.scalar.copy, nc.vector.tensor_copy)):
+            copy(w1_b[pair][:].rearrange("p t m j -> p m t j"), w1_from[:, :, 2 * pair : 2 * pair + 2, :])
         rows = sb("rows", [P, 2, S], F32, "w1_raw")
         for k in range(2):
             nc.scalar.copy(rows[:, k, :], rows_ps[k][:])
-        xs_g = sb("xs_g", [P, S], U8, "inv_pivot")
+        xs_g = sb("xs_g", [P, S], U8, "others")
         nc.vector.tensor_copy(xs_g[:], xs[:].indirect(offs_t[:]))
-        quantize_w1(0, "xs")
-        xw_g = [sb(f"xw_g{h}", [P, HALF], U32) for h in range(2)]
+        w1_q = sb("w1_q", [P, H], U32, "xs")
+        w1_s = sb("w1_s", [P, H], U8)
+        for pair in (1, 0):
+            cols = slice(2 * pair * P, 2 * (pair + 1) * P)
+            nc.vector.quantize_mx(
+                out=w1_q[:, cols].bitcast(FP8X4), scales=w1_s[:, cols],
+                in_=w1_b[pair][:].rearrange("p t m j -> p (t m j)"),
+            )
+        xw_g = sb("xw_g", [P, 2, HALF], U32, "gains")
         for h in range(2):
             nc.vector.tensor_copy(
-                xw_g[h][:],
+                xw_g[:, h, :],
                 xw[:].bitcast(U32).indirect(offs_t[:, h * HALF // LIST_ROWS : (h + 1) * HALF // LIST_ROWS]),
             )
-        quantize_w1(1, "xw")
 
         def first_product(ps, t, lo, width):
             nc.tensor.matmul_mx(
                 out=ps,
-                lhsT=w1_q[t // 2][:, t % 2 * P : (t % 2 + 1) * P].bitcast(FP8X4),
+                lhsT=w1_q[:, t * P : (t + 1) * P].bitcast(FP8X4),
                 lhsT_scale=w1_s[:, t * P : (t + 1) * P],
-                rhs=xw_g[lo // HALF][:, lo % HALF : lo % HALF + width].bitcast(FP8X4),
+                rhs=xw_g[:, lo // HALF, lo % HALF : lo % HALF + width].bitcast(FP8X4),
                 rhs_scale=xs_g[:, lo : lo + width],
                 start=True,
                 stop=True,
@@ -181,13 +167,14 @@ def tile_picked_ace8_none_p_kernel(
 
         w_q = {}
         w_s = [sb(f"w_s{i}", [P, N], U8) for i in range(2)]
-        w3_b = sb("w3_b", [P, N, PACK], BF16, "gains")
+        w3_b = sb("w3_b", [P, N, PACK], BF16, "xw")
         w2_b = {}
 
-        def weave_w2(h, tag):
-            w2_b[h] = sb(f"w2_b{h}", [P, HALF, PACK], BF16, tag)
+        def weave_w2(lo, width, tag):
+            w2_b[lo] = sb(f"w2_b{lo}", [P, width, PACK], BF16, tag)
+            raw = w2_raw[lo // HALF][:, :, lo % HALF : lo % HALF + width]
             nc.scalar.copy(
-                w2_b[h][:].rearrange("p (c i) t -> p c t i", i=4), w2_raw[h][:].rearrange("p t (c i) -> p c t i", i=4)
+                w2_b[lo][:].rearrange("p (c i) t -> p c t i", i=4), raw.rearrange("p t (c i) -> p c t i", i=4)
             )
 
         def weave_w3(h):
@@ -260,7 +247,7 @@ def tile_picked_ace8_none_p_kernel(
         squares_b = sb("squares_b", [P, HALF, PACK], BF16)
         products_b = [sb(f"products_b{b}", [P, P, PACK], BF16) for b in range(2)]
 
-        plain = [sb(f"plain{t}", [P, S], F32) for t in range(PACK)]
+        plain = [sb(f"plain{t}", [P, S if t < 3 else HALF], F32) for t in range(PACK)]
 
         def add_term(term, t, groups, start, stop):
             for i in range(term.shape[1] // P):
@@ -281,7 +268,7 @@ def tile_picked_ace8_none_p_kernel(
             if t + 1 < PACK:
                 empty_plane(t + 1)
             width = S if t < 2 else HALF
-            for lo in range(0, S, width):
+            for lo in range(0, plain[t].shape[1], width):
                 plain_term(plain[t][:, lo : lo + width], t, lo)
         weave_w3(0)
         add_term(plain[0][:], 0, low, True, False)
@@ -295,18 +282,23 @@ def tile_picked_ace8_none_p_kernel(
             sums[b] = bank(2 + b, [P, P, PACK])
         for h in range(2):
             turn_back(low[h], 0, (0, 1), 2 * h)
-        weave_w2(0, "scaled1_0")
+        weave_w2(0, HALF, "scaled1_0")
+        weave_w2(HALF, P, "turned0_0")
         for t in (2, 3):
             unit(t, 0, HALF, high[0:1])
         unit(2, HALF, HALF, high[1:2])
         turn_back(high[0], 2, (0, 1), 0, sb("turned_a", [P, 2, 2, P], F32, "w2_raw0")[:])
+        plain_last = sb("plain_last", [P, HALF], F32, "scaled3_0")
+        plain_term(plain_last[:], 3, HALF)
+        add_term(plain_last[:], 3, high[1:2], False, False)
         unit(3, HALF, HALF, high[1:2])
-        weave_w2(1, "scaled3_0")
         codes = sb("codes", [P, 2, N], U32, "y3")
         w_q[0], w_q[1] = codes[:, 0, :], codes[:, 1, :]
         for b in range(2):
             second_order(squares_a[:, b * P : (b + 1) * P, :], b)
-        turn_back(high[1], 2, (0, 1), 2, sb("turned_b", [P, 2, 2, P], F32, "w2_raw1")[:])
+        turn_back(high[1], 2, (0, 1), 2, sb("turned_b", [P, 2, 2, P], F32, "w2_raw0")[:])
+        weave_w2(HALF + P, P, f"scaled3_{HALF}")
+
         def leave(o_ps, first_tile, name):
             o_sb = sb(name, list(o_ps.shape), F32)
             nc.scalar.copy(o_sb[:], o_ps)
@@ -327,7 +319,8 @@ def tile_picked_ace8_none_p_kernel(
             one_pass(out_a[a][:, 0, :], 0, a, z_a, 0, False, True)
             leave(out_a[a][:], a, f"o_a{a}")
         quantize_weights(1, w3_b[:, HALF:N, :], HALF)
-        quantize_weights(0, w2_b[1][:], HALF)
+        for lo in (HALF, HALF + P):
+            quantize_weights(0, w2_b[lo][:], lo)
         for i, z in ((1, z_sq_a), (0, z_a)):
             for a in range(2):
                 one_pass(out_a[2][:, a, :], i, 2 + a, z, 0, (i, a) == (1, 0), (i, a) == (0, 1))

from contextlib import ExitStack

import concourse.mybir as mybir
from concourse.masks import make_identity

K, T, S, N, H = 512, 2048, 512, 512, 512
FLOPS = 2 * K * H * S + 2 * 2 * H * N * S

F32 = mybir.dt.float32
BF16 = mybir.dt.bfloat16
I32 = mybir.dt.int32
U32 = mybir.dt.uint32
U16 = mybir.dt.uint16
U8 = mybir.dt.uint8
FP8X4 = mybir.dt.float8_e4m3fn_x4
MULT = mybir.AluOpType.mult
MAX = mybir.AluOpType.max
MIN = mybir.AluOpType.min
IS_GE = mybir.AluOpType.is_ge
SUBTRACT = mybir.AluOpType.subtract
COPY = mybir.ActivationFunctionType.Copy
SQUARE = mybir.ActivationFunctionType.Square
SQRT = mybir.ActivationFunctionType.Sqrt

P = 128
PACK = 4
HALF = S // 2
LIST_ROWS = 16
BATCHES = S // P
TINY = 2.0**-110
INV_BOUND = 2.0**63
GPSIMD_CLEARS = 640


def tile_picked_ace8_none_p_kernel(
    tc, x_words, x_scales, w1, g1, g2, g3, c2, c1, w2, w3, offs, p1, p2, p3, out
):
    nc = tc.nc
    with ExitStack() as ctx:
        keep = ctx.enter_context(tc.tile_pool(name="keep", bufs=1))
        psum = ctx.enter_context(tc.psum_pool(name="psum", bufs=1))

        def bank(b, shape):
            return psum.tile(shape, F32, name=f"bank{b}", tag=f"bank{b}")

        def sb(name, shape, dtype, tag=None):
            return keep.tile(shape, dtype, name=name, tag=tag or name, align_bytes=64)

        def load_list(name, src):
            lt = keep.tile([P, S // LIST_ROWS], U16, name=name)
            nc.sync.dma_start(lt[:], src)
            return lt

        def load_factor(name, src):
            ct = keep.tile([P, PACK], F32, name=name)
            nc.sync.dma_start(ct[:], src.rearrange("(p t) o -> p (t o)", t=PACK))
            return ct

        gains = sb("gains", [P, P], F32)
        for src, lo, hi in ((g1, 0, 64), (g2, 64, 96), (g3, 96, 128)):
            nc.scalar.dma_start(gains[lo:hi, :], src.rearrange("r (b c) -> (r b) c", c=P)[0 : hi - lo, :])
        xs = sb("xs", [P, T], U8)
        nc.gpsimd.memset(xs[:, 0:GPSIMD_CLEARS].bitcast(I32), 0)
        nc.vector.memset(xs[:, GPSIMD_CLEARS:T].bitcast(I32), 0)
        offs_t = load_list("offs_t", offs)
        c2_t = load_factor("c2_t", c2)
        c1_t = load_factor("c1_t", c1)
        w1_raw = sb("w1_raw", [P, PACK, H], F32)
        nc.sync.dma_start(w1_raw[:], w1.rearrange("(p j) c -> p j c", j=PACK))
        for i in range(4):
            nc.sync.dma_start(xs[i:P:32, :].bitcast(I32), x_scales[0, i:16:4, :].bitcast(I32))
        xw = sb("xw", [P, T], I32)
        nc.sync.dma_start(xw[:], x_words[0].rearrange("p n t -> p (n t)").bitcast(I32))
        w3_rows = w3.rearrange("(p j) c -> p j c", j=PACK)
        w3_raw = [sb(f"w3_raw{i}", [P, PACK, HALF], F32) for i in range(2)]
        nc.sync.dma_start(w3_raw[0][:], w3_rows[:, :, 0:HALF])
        lists = [load_list(f"list{k}", src) for k, src in enumerate((p1, p2, p3))]
        nc.sync.dma_start(w3_raw[1][:], w3_rows[:, :, HALF:N])
        w2_rows = w2.rearrange("(p j) c -> p j c", j=PACK)
        w2_raw = [sb(f"w2_raw{i}", [P, PACK, HALF], F32) for i in range(2)]
        for i in range(2):
            nc.sync.dma_start(w2_raw[i][:], w2_rows[:, :, i * HALF : (i + 1) * HALF])

        ident = keep.tile([P, P], F32, name="ident")
        make_identity(nc, ident[:])

        mag, root, not_below, sign, inv_root = (
            sb(name, [P, PACK], F32) for name in ("mag", "root", "not_below", "sign", "inv_root")
        )
        nc.vector.scalar_tensor_tensor(mag[:], c2_t[:], -1.0, c2_t[:], MULT, MAX)
        nc.scalar.activation(root[:], mag[:], SQRT, bias=TINY)
        nc.vector.tensor_scalar(not_below[:], c2_t[:], 0.0, 2.0, IS_GE, MULT)
        nc.vector.tensor_scalar(sign[:], not_below[:], 1.0, None, SUBTRACT)
        nc.vector.reciprocal(inv_root[:], root[:])
        ratio = sb("ratio", [P, PACK], F32)
        nc.vector.tensor_tensor(ratio[:], c1_t[:], inv_root[:], MULT)

        gains_ps = bank(0, [P, P])
        nc.tensor.transpose(gains_ps[:], gains[:], ident[:])
        g_cols = gains_ps[:, 32:P].rearrange("p (k q) -> p k q", q=32)[:, :, 0:BATCHES]
        inv_gain, inv_pivot, pivot = (sb(name, [P, BATCHES], F32) for name in ("inv_gain", "inv_pivot", "pivot"))
        others, quot = (sb(name, [P, 2, BATCHES], F32) for name in ("others", "quot"))
        nc.vector.reciprocal(inv_gain[:], g_cols[:, 0, :])
        nc.vector.tensor_copy(others[:], g_cols[:, 1:3, :])
        nc.vector.tensor_scalar(inv_pivot[:], inv_gain[:], INV_BOUND, -INV_BOUND, MIN, MAX)
        nc.vector.reciprocal(pivot[:], inv_pivot[:])
        nc.vector.tensor_tensor(
            quot[:], others[:], inv_pivot[:].unsqueeze(1).to_broadcast([P, 2, BATCHES]), MULT
        )
        rows_ps = [bank(6 + k, [P, S]) for k in range(2)]
        for k in range(2):
            for b in range(BATCHES):
                nc.tensor.transpose(
                    rows_ps[k][:, b * P : (b + 1) * P], quot[:, k, b : b + 1].to_broadcast([P, P]), ident[:]
                )

        w1_from = w1_raw[:].rearrange("p j (m t) -> p m t j", t=PACK)
        w1_b = [sb(f"w1_b{pair}", [P, 2, P, PACK], BF16, tag) for pair, tag in enumerate(("gains", "inv_pivot"))]
        for pair, copy in enumerate((nc.scalar.copy, nc.vector.tensor_copy)):
            copy(w1_b[pair][:].rearrange("p t m j -> p m t j"), w1_from[:, :, 2 * pair : 2 * pair + 2, :])
        rows = sb("rows", [P, 2, S], F32, "w1_raw")
        for k in range(2):
            nc.scalar.copy(rows[:, k, :], rows_ps[k][:])
        xs_g = sb("xs_g", [P, S], U8, "others")
        nc.vector.tensor_copy(xs_g[:], xs[:].indirect(offs_t[:]))
        w1_q = sb("w1_q", [P, H], U32, "xs")
        w1_s = sb("w1_s", [P, H], U8)
        for pair in (1, 0):
            cols = slice(2 * pair * P, 2 * (pair + 1) * P)
            nc.vector.quantize_mx(
                out=w1_q[:, cols].bitcast(FP8X4), scales=w1_s[:, cols],
                in_=w1_b[pair][:].rearrange("p t m j -> p (t m j)"),
            )
        xw_g = sb("xw_g", [P, 2, HALF], U32, "gains")
        for h in range(2):
            nc.vector.tensor_copy(
                xw_g[:, h, :],
                xw[:].bitcast(U32).indirect(offs_t[:, h * HALF // LIST_ROWS : (h + 1) * HALF // LIST_ROWS]),
            )

        def first_product(ps, t, lo, width):
            nc.tensor.matmul_mx(
                out=ps,
                lhsT=w1_q[:, t * P : (t + 1) * P].bitcast(FP8X4),
                lhsT_scale=w1_s[:, t * P : (t + 1) * P],
                rhs=xw_g[:, lo // HALF, lo % HALF : lo % HALF + width].bitcast(FP8X4),
                rhs_scale=xs_g[:, lo : lo + width],
                start=True,
                stop=True,
            )

        y = [sb(f"y{t}", [P, 2 * S if t < 2 else S], F32) for t in range(PACK)]
        for t in range(2):
            nc.vector.memset(y[t][:, S : 2 * S].bitcast(I32), 0)
        for b, lo, width in ((0, 0, HALF), (1, HALF, P), (3, HALF + P, P)):
            ps = bank(b, [P, width])
            first_product(ps[:], 0, lo, width)
            nc.scalar.activation(y[0][:, lo : lo + width], ps[:], COPY, scale=root[:, 0:1])
        y_ps = {}
        for t, b in zip(range(1, PACK), (4, 5, 2)):
            y_ps[t] = bank(b, [P, S])
            for lo in (HALF, 0):
                first_product(y_ps[t][:, lo : lo + HALF], t, lo, HALF)

        def empty_plane(t):
            nc.scalar.activation(y[t][:, 0:S], y_ps[t][:], COPY, scale=root[:, t : t + 1])

        w_q = {}
        w_s = [sb(f"w_s{i}", [P, N], U8) for i in range(2)]
        w3_b = sb("w3_b", [P, N, PACK], BF16, "xw")
        w2_b = {}

        def weave_w2(lo, width, tag):
            w2_b[lo] = sb(f"w2_b{lo}", [P, width, PACK], BF16, tag)
            raw = w2_raw[lo // HALF][:, :, lo % HALF : lo % HALF + width]
            nc.scalar.copy(
                w2_b[lo][:].rearrange("p (c i) t -> p c t i", i=4), raw.rearrange("p t (c i) -> p c t i", i=4)
            )

        def weave_w3(h):
            nc.vector.tensor_tensor(
                w3_b[:, h * HALF : (h + 1) * HALF, :].rearrange("p (c i) t -> p c t i", i=4),
                w3_raw[h][:].rearrange("p t (c i) -> p c t i", i=4),
                sign[:].unsqueeze(1).unsqueeze(3).to_broadcast([P, HALF // 4, PACK, 4]), MULT,
            )

        def quantize_weights(i, woven, lo):
            cols = slice(lo, lo + woven.shape[1])
            nc.vector.quantize_mx(
                out=w_q[i][:, cols].bitcast(FP8X4), scales=w_s[i][:, cols], in_=woven.rearrange("p m t -> p (m t)")
            )

        def offsets(k, lo, width):
            return lists[k][:, lo // LIST_ROWS : (lo + width) // LIST_ROWS]

        def plain_term(dst, t, lo):
            nc.scalar.activation(dst, y[t][:].indirect(offsets(0, lo, dst.shape[1])), COPY)

        def scaled_term(dst, t, k, lo):
            width = dst.shape[1]
            nc.vector.tensor_tensor(
                dst, y[t][:].indirect(offsets(k, lo, width)), rows[:, k - 1, lo : lo + width], MULT
            )

        def turn_back(ps, plane, which, first, turned=None):
            planes = ps.shape[2]
            if turned is None:
                turned = sb(f"turned{plane}_{first}", [P, len(which), planes, P], F32)[:]
            for n, i in enumerate(which):
                b = first + i
                nc.scalar.activation(turned[:, n], ps[:, i], COPY, scale=pivot[:, b : b + 1])
                for slot in range(planes):
                    nc.tensor.transpose(sums[b][:, :, plane + slot], turned[:, n, slot, :], ident[:])

        def first_order(dst, b):
            nc.vector.tensor_tensor(
                dst, sums[b][:],
                ratio[:].unsqueeze(1).to_broadcast([P, P, PACK]), MULT,
            )

        def second_order(dst, b):
            nc.scalar.activation(dst, sums[b][:], SQUARE)

        def quantize_values(name, values):
            width = values.shape[1] // PACK
            zq = sb(f"zq{name}", [P, width], U32)
            zs = sb(f"zs{name}", [P, width], U8)
            nc.vector.quantize_mx(out=zq[:].bitcast(FP8X4), scales=zs[:], in_=values)
            return zq, zs

        def one_pass(o_ps, i, a, z, lo, start, stop):
            width = o_ps.shape[1]
            nc.tensor.matmul_mx(
                out=o_ps,
                lhsT=w_q[i][:, a * P : (a + 1) * P].bitcast(FP8X4),
                lhsT_scale=w_s[i][:, a * P : (a + 1) * P],
                rhs=z[0][:, lo : lo + width].bitcast(FP8X4),
                rhs_scale=z[1][:, lo : lo + width],
                start=start,
                stop=stop,
            )

        out_v = out.rearrange("(a p) j -> p a j", p=P)
        sums = {}
        squares_a = sb("squares_a", [P, HALF, PACK], BF16)
        products_a = sb("products_a", [P, HALF, PACK], BF16)
        squares_b = sb("squares_b", [P, HALF, PACK], BF16)
        products_b = [sb(f"products_b{b}", [P, P, PACK], BF16) for b in range(2)]

        plain = [sb(f"plain{t}", [P, S if t < 3 else HALF], F32) for t in range(PACK)]

        def add_term(term, t, groups, start, stop):
            for i in range(term.shape[1] // P):
                nc.tensor.matmul(
                    groups[i // 2][:, i % 2, t % 2, :], term[:, i * P : (i + 1) * P], ident[:],
                    start=start and i % 2 == 0, stop=stop and i % 2 == 1, is_transpose=True,
                )

        def unit(t, lo, width, groups):
            scaled = sb(f"scaled{t}_{lo}", [P, 2, width], F32)
            for k in (1, 2):
                scaled_term(scaled[:, k - 1, :], t, k, lo)
                add_term(scaled[:, k - 1, :], t, groups, False, t % 2 == 1 and k == 2)

        low = [bank(h, [P, 2, 2, P]) for h in range(2)]
        high = [bank(6 + h, [P, 2, 2, P]) for h in range(2)]
        for t in range(PACK):
            if t + 1 < PACK:
                empty_plane(t + 1)
            width = S if t < 2 else HALF
            for lo in range(0, plain[t].shape[1], width):
                plain_term(plain[t][:, lo : lo + width], t, lo)
        weave_w3(0)
        add_term(plain[0][:], 0, low, True, False)
        unit(0, 0, S, low)
        weave_w3(1)
        add_term(plain[1][:], 1, low, False, False)
        add_term(plain[2][:], 2, high, True, False)
        unit(1, 0, S, low)
        add_term(plain[3][:], 3, high, False, False)
        for b in range(BATCHES):
            sums[b] = bank(2 + b, [P, P, PACK])
        for h in range(2):
            turn_back(low[h], 0, (0, 1), 2 * h)
        weave_w2(0, HALF, "scaled1_0")
        weave_w2(HALF, P, "turned0_0")
        for t in (2, 3):
            unit(t, 0, HALF, high[0:1])
        unit(2, HALF, HALF, high[1:2])
        turn_back(high[0], 2, (0, 1), 0, sb("turned_a", [P, 2, 2, P], F32, "w2_raw0")[:])
        plain_last = sb("plain_last", [P, HALF], F32, "scaled3_0")
        plain_term(plain_last[:], 3, HALF)
        add_term(plain_last[:], 3, high[1:2], False, False)
        unit(3, HALF, HALF, high[1:2])
        codes = sb("codes", [P, 2, N], U32, "y3")
        w_q[0], w_q[1] = codes[:, 0, :], codes[:, 1, :]
        for b in range(2):
            second_order(squares_a[:, b * P : (b + 1) * P, :], b)
        turn_back(high[1], 2, (0, 1), 2, sb("turned_b", [P, 2, 2, P], F32, "w2_raw0")[:])
        weave_w2(HALF + P, P, f"scaled3_{HALF}")

        def leave(o_ps, first_tile, name):
            o_sb = sb(name, list(o_ps.shape), F32)
            nc.scalar.copy(o_sb[:], o_ps)
            nc.sync.dma_start(out_v[:, first_tile : first_tile + o_ps.shape[1], 0:HALF], o_sb[:])

        quantize_weights(1, w3_b[:, 0:HALF, :], 0)
        first_order(products_a[:, 0:P, :], 0)
        out_a = [bank(0, [P, 1, HALF]), bank(1, [P, 1, HALF]), bank(6, [P, 2, HALF])]
        z_sq_a = quantize_values("a1", squares_a[:].rearrange("p j t -> p (j t)"))
        for a in range(2):
            one_pass(out_a[a][:, 0, :], 1, a, z_sq_a, 0, True, False)
        first_order(products_a[:, P:HALF, :], 1)
        quantize_weights(0, w2_b[0][:], 0)
        z_a = quantize_values("a0", products_a[:].rearrange("p j t -> p (j t)"))
        for b in range(2):
            second_order(squares_b[:, b * P : (b + 1) * P, :], 2 + b)
        for a in range(2):
            one_pass(out_a[a][:, 0, :], 0, a, z_a, 0, False, True)
            leave(out_a[a][:], a, f"o_a{a}")
        quantize_weights(1, w3_b[:, HALF:N, :], HALF)
        for lo in (HALF, HALF + P):
            quantize_weights(0, w2_b[lo][:], lo)
        for i, z in ((1, z_sq_a), (0, z_a)):
            for a in range(2):
                one_pass(out_a[2][:, a, :], i, 2 + a, z, 0, (i, a) == (1, 0), (i, a) == (0, 1))
        leave(out_a[2][:], 2, "o_a2")
        first_order(products_b[0][:], 2)
        z_sq = quantize_values("b_squares", squares_b[:].rearrange("p j t -> p (j t)"))
        first_order(products_b[1][:], 3)
        out_b = [[bank(n, [P, 2, P]) for n in banks] for banks in ((7, 2), (3, 0))]
        for b in range(2):
            for a in range(4):
                one_pass(out_b[b][a // 2][:, a % 2, :], 1, a, z_sq, b * P, a % 2 == 0, False)
        for b in range(2):
            z_b = quantize_values(f"b{b}", products_b[b][:].rearrange("p j t -> p (j t)"))
            for pair, copy in enumerate((nc.scalar.copy, nc.vector.tensor_copy)):
                for a in range(2):
                    one_pass(out_b[b][pair][:, a, :], 0, 2 * pair + a, z_b, 0, False, a == 1)
                o_sb = sb(f"o_b{b}_{pair}", [P, 2, P], F32)
                copy(o_sb[:], out_b[b][pair][:])
                first = HALF + b * P
                nc.sync.dma_start(out_v[:, 2 * pair : 2 * pair + 2, first : first + P], o_sb[:])
